import numpy as np, ml_dtypes
CORES = [24,25,26,27,28,29,30,31]
N = 8
BF = ml_dtypes.bfloat16
def gentries(a):
    return np.ascontiguousarray(a.reshape(8, 16, -1).transpose(0, 2, 1)).reshape(8, -1)
def gtable(e):
    e = np.asarray(e); return np.ascontiguousarray(e.reshape(8, -1, 16).transpose(0, 2, 1)).reshape(128, -1).astype(np.int32)
TP, C, W, S, Q, P, B = 8, 384, 2048, 5, 3, 4, 512
CB = C // P
def sign(rng, *shape):
    return 1.0 - 2.0 * rng.integers(0, 2, shape)
def draw_lists(rng):
    nt = np.ascontiguousarray(np.argsort(rng.random((N, 8, S, W)), axis=-1)[..., :C])
    return rng.integers(0, W, (N, 8, TP, C)), rng.integers(0, W, (N, 8, Q, C)), nt
def draw_floats(rng):
    w = rng.standard_normal((N, 8, 16, TP, C), dtype=np.float32) * 0.25 * np.exp2(rng.integers(-1, 2, (N, 8, 1, TP, C)).astype(np.float32))
    r = rng.standard_normal((N, 8, 16, W), dtype=np.float32) * np.exp2(rng.integers(-1, 2, (N, 8, 16, 1)).astype(np.float32))
    d = rng.standard_normal((N, 8, 16, S, C), dtype=np.float32) * np.exp2(rng.integers(-1, 2, (N, 8, 16, 1, 1)).astype(np.float32))
    return w, r, d
def wide(rng, v, lo, hi):
    k = v.shape[:2] + (1,) + v.shape[3:]
    return v * np.exp2(rng.integers(lo, hi + 1, k).astype(np.float32)) * (rng.random(k) > 0.0625)
def pack(w, r, d, dl, qu, nt):
    b = lambda v: np.ascontiguousarray(np.clip(np.where(np.abs(v) < 2.0 ** -20, 0, v), -8, 8).reshape(N, 128, -1)).astype(np.float32).astype(BF)
    i = lambda v: np.stack([gtable(a.reshape(8, -1)) for a in v])
    return {"w0": b(w), "r0": b(r), "d0": b(d), "dl": i(dl), "qu": i(qu), "nt": i(nt)}
def kinds(rng):
    return ((np.arange(8) + np.arange(N)[:, None] + rng.integers(0, 4)) & 3).reshape(N, 8, 1, 1)
def plant(v, c, wt, x, des, tap, off):
    w, r, d, dl, qu, nt = v; col = W // 2 + TP * c + np.arange(TP)
    dl[:, :, :, c] = (nt[:, :, 0, c][:, :, None] - col) & (W - 1)
    qu[:, :, 0, c] = (dl[:, :, tap, c] + off) & (W - 1)
    w[..., c] = wt; r[..., col] = x; d[:, :, :, 0, c] = des
def setup_inputs(rng):
    w, r, d = draw_floats(rng); dl, qu, nt = draw_lists(rng)
    return pack(w, r, d, dl, qu, nt)
def setup_inputs_spread(rng):
    w, r, d = draw_floats(rng); dl, qu, nt = draw_lists(rng)
    return pack(wide(rng, w, -2, 2), wide(rng, r, -2, 2), wide(rng, d, -2, 2), dl, qu, nt)
def setup_inputs_ends(rng):
    w, r, d = draw_floats(rng); dr, qr, nt = draw_lists(rng)
    free = rng.random((N, 8, 1, C)) < 0.25; free[..., 0] = False; free[..., C - 1] = False
    dl = np.where(free, dr, rng.integers(0, 2, (N, 8, TP, C)) * (W - 1)); qu = np.where(free, qr, rng.integers(0, 2, (N, 8, Q, C)) * (W - 1))
    pool = np.concatenate([np.arange(C // 2), W - C // 2 + np.arange(C // 2)]); rest = pool[(pool != 1) & (pool != W - 1)]
    nt = pool[np.argsort(rng.random((N, 8, S, C)), axis=-1)]
    nt[:, :, 0, 1:C - 1] = rest[np.argsort(rng.random((N, 8, C - 2)), axis=-1)]; nt[:, :, 0, 0] = 1; nt[:, :, 0, C - 1] = W - 1
    w = np.where(rng.random((N, 8, 1, 1, C)) < 0.3, 8.0 * sign(rng, N, 8, 16, TP, C), w); w[..., C - 1] = 8.0; w[..., 0] = -8.0
    r = np.where(rng.random((N, 8, 1, W)) < 0.3, 8.0 * sign(rng, N, 8, 16, W), r)
    for j in (0, 1, 2, W - 1): r[..., j] = 8.0
    d = np.where(rng.random((N, 8, 1, S, C)) < 0.4, 8.0 * sign(rng, N, 8, 16, S, C), d); d[:, :, :, 0, C - 1] = -8.0; d[:, :, :, 0, 0] = 8.0
    v = (w, r, d, dl, qu, nt)
    u = 7.0 + rng.random((N, 8, 16, TP // 2))
    plant(v, 1, np.concatenate([u, -u], axis=3), 8.0, np.where(rng.random((N, 8, 16)) < 0.25, 0.0, 2.0 * rng.random((N, 8, 16)) - 1.0), 0, 0)
    x = 2.0 ** -6 + 2.0 ** -7 * rng.random((N, 8, 16, TP)); x[..., 4] = 2.0 ** -7; x[..., 2] = 2.0 ** -5; u = sign(rng, N, 8, 16, TP)
    plant(v, 2, 8.0 * u, x * u, 8.0, 2, 0)
    return pack(*v)
def setup_inputs_crowd(rng):
    w, r, d = draw_floats(rng); dl, qu, nt = draw_lists(rng); r = np.clip(r, -2, 2); kind = kinds(rng)
    row = np.arange(16).reshape(1, 1, 16, 1); tap = np.arange(TP).reshape(TP, 1)
    four = np.argsort(rng.random((N, 8, TP, C)), axis=2)[:, :, :4, None]
    turn = (row + rng.integers(0, 16, (N, 8, 1, C))) & 15
    other = np.where(kind == 1, turn == 0, (kind == 2) & (turn < 8))
    lo = np.where(other, four[:, :, 1], four[:, :, 0]); hi = np.where(other, four[:, :, 3], four[:, :, 2])
    w = sign(rng, N, 8, 16, TP, C) * (0.5 + 0.5 * rng.random((N, 8, 16, TP, C)))
    w = np.where(tap == lo[:, :, :, None], 0.0, w); w = np.where(tap == hi[:, :, :, None], 2.0 * sign(rng, N, 8, 16, TP, C), w)
    w = np.where(kind[..., None] == 3, sign(rng, N, 8, 16, 1, C) * (0.5 + 0.5 * rng.random((N, 8, 16, 1, C))), w)
    dl = np.where(kind == 3, dl[:, :, :1], dl)
    v = (w, r, d, dl, qu, nt)
    odd = np.arange(16) == rng.integers(0, 16, (N, 8, 1))
    u = sign(rng, N, 8, 16, TP) * (0.5 + 0.5 * rng.random((N, 8, 16, TP)))
    u[..., 1] = np.where(odd, 0.5, 0.125); u[..., 4] = 0.125; u[..., 2] = np.where(odd, 1.0, 2.0); u[..., 6] = 2.0
    plant(v, 0, u, 0.5 + rng.random((N, 8, 16, 1)), 2.0 * rng.random((N, 8, 16)) - 1.0, 6, -B)
    u = sign(rng, N, 8, 16, TP) * (1.5 + 0.5 * rng.random((N, 8, 16, TP))); x = 2.0 ** -4 * sign(rng, N, 8, 16, TP)
    u[..., 1] = 1.0; u[..., 4] = 1.0; u[..., 2] = 3.0; u[..., 6] = 3.0
    x[..., 1] = 1.5 * 2.0 ** -20; x[..., 4] = 2.0 ** -20; x[..., 2] = 2.0 ** -20; x[..., 6] = 1.5 * 2.0 ** -20
    plant(v, 1, u, x, 8.0, 2, B)
    return pack(*v)
def setup_inputs_corners(rng):
    w, r, d = draw_floats(rng); dl, qu, nt = draw_lists(rng); kind = kinds(rng); half = rng.random((N, 8, 1, C)) < 0.5
    w = np.where(kind[..., None] == 0, 0.0, w); dl = np.where((kind == 0) & half, dl[:, :, :1], dl)
    one = rng.integers(0, W, (N, 8, 1, C)); far = np.where(half, one, (one + W // 2) & (W - 1))
    dl = np.where(kind == 1, one, dl); qu = np.where(kind == 1, far, qu)
    few = rng.choice(np.array([0, 1, W // 2, W - 1]), (N, 8, Q, C)); qu = np.where(kind >= 2, few, qu)
    first = nt[:, :, :1]; nt = np.where(kind == 2, (first + np.arange(S)[:, None]) & (W - 1), np.where(kind == 3, first, nt))
    near = 1 + rng.integers(0, S, (N, 8, TP, C)); own = np.where(rng.random((N, 8, TP, C)) < 0.5, 0, rng.choice(np.array([0, 1, W // 2, W - 1]), (N, 8, TP, C)))
    dl = np.where(kind == 2, near, np.where(kind == 3, own, dl))
    v = (w, r, d, dl, qu, nt)
    u = np.zeros((N, 8, 16, TP)); u[..., 0] = 2.0 ** -16; x = 2.0 + 6.0 * rng.random((N, 8, 16, TP)); x[..., 0] = 2.0 ** -17; x[..., 4] = 1.0
    plant(v, 0, u, x, 0.0, 0, 0)
    u = sign(rng, N, 8, 16, TP) * (3.0 + rng.random((N, 8, 16, TP))); x = 2.0 ** -5 * sign(rng, N, 8, 16, TP)
    u[..., 1] = 1.9921875; u[..., 4] = 1.9921875; u[..., 2] = 6.0; x[..., 1] = 3.0 * 2.0 ** -18; x[..., 4] = 2.0 ** -17
    plant(v, 1, u, x, 8.0, 2, 0)
    return pack(*v)
def setup_inputs_edge(rng):
    w, r, d = draw_floats(rng); dl, qu, nt = draw_lists(rng); r = np.clip(r, -2, 2); w = np.clip(w, -0.5, 0.5)
    tap = np.arange(TP).reshape(TP, 1); k = rng.integers(0, TP, (N, 8, 1, C)); base = rng.integers(0, W, (N, 8, 1, C))
    w = np.where(tap == k[:, :, None], 1.5 * sign(rng, N, 8, 16, 1, C), w)
    away = np.array([B - 1, B, B + 1, 1 - B, -B, -B - 1, 0, W // 2])
    dl = np.where(tap == k, base, (base + rng.choice(away, (N, 8, TP, C))) & (W - 1)); qu = (base + rng.choice(away, (N, 8, Q, C))) & (W - 1)
    v = (w, r, d, dl, qu, nt)
    side = sign(rng, N, 8, 16); way = side * sign(rng, N, 8, 16)
    u = np.zeros((N, 8, 16, TP)); x = 1.0 + rng.random((N, 8, 16, TP))
    u[..., 0] = 7.5 * side; u[..., 1] = 1.5 * 2.0 ** -10 * way; u[..., 2] = -7.5 * side; u[..., 3] = -(2.0 ** -10) * way
    x[..., 0] = 8.0; x[..., 1] = 2.0 ** -10; x[..., 2] = 8.0; x[..., 3] = 2.0 ** -10
    plant(v, 0, u, x, 2.0 * side, 0, 0)
    return pack(*v)
def check_inputs(d):
    bad = []
    for k in ("dl", "qu", "nt"):
        if np.min(d[k]) < 0 or np.max(d[k]) > W - 1: bad.append("range of " + k)
    for k in ("w0", "r0", "d0"):
        m = np.abs(np.asarray(d[k]).astype(np.float32))
        if not np.all((m <= 8) & ((m == 0) | (m >= 2.0 ** -20))): bad.append("size of " + k)
    n = np.sort(np.stack([gentries(a) for a in d["nt"]]).reshape(N, 8, S, C), axis=-1)
    if np.any(n[..., 1:] == n[..., :-1]): bad.append("times of a step differ")
    return bad
def reference(w0, r0, d0, dl, qu, nt):
    w = w0.astype(np.float32).reshape(N, 8, 16, TP, C); r = r0.astype(np.float32).reshape(N, 8, 16, W); d = d0.astype(np.float32).reshape(N, 8, 16, S, C)
    a = np.stack([gentries(v) for v in dl]).astype(np.int64).reshape(N, 8, TP, C)
    q = np.stack([gentries(v) for v in qu]).astype(np.int64).reshape(N, 8, Q, C)
    n = np.stack([gentries(v) for v in nt]).astype(np.int64).reshape(N, 8, S, C)
    tap = np.arange(TP).reshape(TP, 1)
    for s in range(S):
        t = n[:, :, s]
        ix = (t[:, :, None] - a) & (W - 1)
        x = np.take_along_axis(r, ix.reshape(N, 8, 1, TP * C), 3).reshape(N, 8, 16, TP, C)
        p = w * x; y = p[:, :, :, 0]
        for k in range(1, TP): y = y + p[:, :, :, k]
        e = np.minimum(np.maximum(d[:, :, :, s] - y, np.float32(-2)), np.float32(2))
        w = w + np.float32(0.015625) * (e[:, :, :, None] * x)
        m = np.abs(w)
        least = np.add.reduce((m == np.min(m, axis=3, keepdims=True)).astype(np.int64), axis=2)
        most = np.add.reduce((m == np.max(m, axis=3, keepdims=True)).astype(np.int64), axis=2)
        weak = np.argmax(least, axis=2)[:, :, None]; strong = np.argmax(most, axis=2)[:, :, None]
        head = q[:, :, s % Q][:, :, None].copy()
        gap = (head - np.take_along_axis(a, strong, 2)) & (W - 1)
        ok = np.minimum(gap, W - gap) <= B
        q[:, :, s % Q] = np.where(ok, np.take_along_axis(a, weak, 2), head)[:, :, 0]
        hit = ok & (tap == weak)
        a = np.where(hit, head, a); w = np.where(hit[:, :, None], np.float32(0.25), w)
        come = np.concatenate([np.roll(np.roll(e[..., b * CB:(b + 1) * CB], 1 + b, axis=0), 1 + s, axis=1) for b in range(P)], axis=3)
        np.put_along_axis(r, t[:, :, None], come, 3)
    q = np.roll(q, -(S % Q), axis=2)
    return {"yw": np.ascontiguousarray(w.reshape(N, 128, TP * C)), "yr": np.ascontiguousarray(come.reshape(N, 128, C)),
            "yd": np.stack([gtable(v.reshape(8, -1)) for v in a]).astype(np.float32), "yq": np.stack([gtable(v.reshape(8, -1)) for v in q]).astype(np.float32)}

@@ -1,0 +1,640 @@
+from concourse.bass import DstId, RemoteDMATransfer
+from concourse.mybir import AluOpType as A, ActivationFunctionType as F, AxisListType
+
+S, H, NB = 5, 2, 192
+PE_UPD = (2, 3)
+DMA_UPD = ()
+GDMA = 1000.0
+S_SCAT = True
+PE_MOD = False
+PE_X = True
+E_PSUM = False
+V_GATH = ((1, 3), (1,))
+TRANS = True
+CY, PCY, LAM = 1.0, 0.5, 170.0
+GATH, SCAT = 1.55, 3.8
+LOOK = {"v": 150.0, "s": 150.0, "t": 600.0}
+LEAD = {'y:w': 13300, 's:snd': -16800, 's:bc': -19000, 'v:p': 1200, 'v:vall': 4400, 's:ssb': -34300, 's:m': 2700, 's:pb4:0': 1500, 's:pb7:1': 7700, 't:pb2': 12800, 't:pb4:2': -21100, 's:sg': -9800, 'v:w': 4500, 's:pb6:1': -17700, 's:x': -2900, 't:x': -10200, 'v:es': -500, 'v:rr': -1800, 'v:pb5': -1900, 's:aa': 7900, 'v:tc': 11100, 't:pb0:2': 3600, 'v:gg': -1400, 'v:ui': 19700, 's:pb0:0': 23400, 'v:td': 10900, 's:ab': 53700, 'v:nh': 26600, 's:w': -14500, 's:pb4:1': 28600, 'v:yds': -5000, 'v:tb': 14300, 'v:ta': 3800, 'v:off': 9600, 's:pb2': 3800, 's:qa': -4100, 't:pb6:0': -9900, 'v:cd': -6200, 't:base': -14500, 's:renew': -21900, 't:load': 1300, 's:xall': -5900, 'v:uj': 11600, 'v:eq': 200, 'v:x': 23000, 't:pb7:0': 1800, 'v:t': -900, 'v:wo': 5800, 'g:t8c': 1400, 'v:quart': -800, 'g:snd': 1000, 'v:t8a': -4000, 'g:offc': -9300, 'v:nidf': -6300, 'g:e2': -2100, 'y:yds': 1500, 'v:ec': -1400, 'v:idb': 3000, 'v:z2': -300, 's:zb': -1300, 'g:za': -600, 'y:land': 10300, 'g:t8b': -7100, 'v:e1': 1200, 'v:ones': 9300, 'v:za': -600, 'v:offc': 4700, 'v:jf': 3300, 'None:land': 2800, 'g:rr': 11600, 'v:idf': -2700, 'v:zb': 3400, 'v:qa': -1500, 'v:i64': -2500, 'g:e1': -5800, 'g:e3': -300, 'v:e2': 1300}
+
+f32, bf16, i32, u16 = "float32", "bfloat16", "int32", "uint16"
+SCRATCH = {
+    "rb": ("sbuf", [128, 2048], bf16), "rr": ("sbuf", [128, 2048], f32), "wb": ("sbuf", [128, 3072], bf16),
+    "db": ("sbuf", [128, 1920], bf16), "dli": ("sbuf", [128, 8, 24], i32), "nti": ("sbuf", [128, 120], i32),
+    "qui": ("sbuf", [128, 72], i32), "ntu": ("sbuf", [128, 120], u16), "qa": ("sbuf", [128, 192], f32),
+    "cd": ("sbuf", [128, 288], f32), "vall": ("sbuf", [128, 8, 144], f32), "xall": ("sbuf", [128, 8, 120], f32),
+    "yds": ("sbuf", [128, 8, 24], f32), "snd": ("sbuf", [128, 1920], f32), "land": ("sbuf", [128, 1920], f32),
+    "ones": ("sbuf", [128, 128], f32), "idf": ("sbuf", [128, 256], f32), "nidf": ("sbuf", [128, 128], f32),
+    "i64": ("sbuf", [128, 128], f32), "idb": ("sbuf", [128, 128], bf16), "idn": ("sbuf", [128, 128], bf16),
+    "z2": ("sbuf", [128, 144], bf16), "t8a": ("sbuf", [128, 8], f32), "t8b": ("sbuf", [128, 8], f32),
+    "t8c": ("sbuf", [128, 8], f32), "pj": ("sbuf", [128, 4], i32), "pk": ("sbuf", [128, 4], i32), "jf": ("sbuf", [128, 4], f32),
+    "e1": ("sbuf", [128, 192], f32), "e2": ("sbuf", [128, 192], f32), "e3": ("sbuf", [128, 192], f32),
+    "ec": ("sbuf", [128, 192], f32), "offc": ("sbuf", [128, 96], f32), "lb": ("sbuf", [128, 12], f32),
+    "lc": ("sbuf", [128, 12], f32), "ld": ("sbuf", [128, 12], f32), "quart": ("sbuf", [128, 192], f32),
+    "za": ("sbuf", [128, 256], f32), "zb": ("sbuf", [128, 256], f32), "idk": ("sbuf", [128, 128], bf16), "kil": ("sbuf", [128, 96], bf16),
+}
+for _h in range(H):
+    for _n, _c, _d in (("w", 1728, f32), ("x", 1536, f32), ("p", 1536, f32), ("t", 1536, f32), ("m", 1536, f32),
+                       ("eq", 3072, bf16), ("es", 192, f32), ("off", 96, u16), ("ui", 96, i32), ("uj", 96, i32),
+                       ("ssb", 96, f32), ("ta", 96, f32), ("tb", 48, f32), ("tc", 24, i32), ("td", 24, i32),
+                       ("gg", 16, f32), ("wo", 12, u16), ("nh", 96, f32), ("bc", 192, f32), ("aa", 96, f32),
+                       ("ab", 96, f32), ("sg", 96, bf16), ("su", 96, bf16), ("ll", 12, u16)):
+        SCRATCH[_n + "_%d" % _h] = ("sbuf", [128, _c], _d)
+for _b in range(8):
+    SCRATCH["pb%d" % _b] = ("psum", [128, 512], f32)
+
+LOADS = ["l_rb", "l_dl", "l_nt", "l_qu", "l_w0", "l_w1", "l_w2", "l_w3", "l_d0", "l_d1", "l_rr"]
+SEMAPHORES = ["ev", "es", "et", "eg", "sent", "out"] + LOADS + ["arr%d_%d" % (s, h) for s in range(S) for h in range(H)]
+SEMAPHORES += ["upd%d_%d_%d" % (s, h, i) for s in range(1, S) for h in range(H) for i in DMA_UPD]
+ESEM = {"v": "ev", "s": "es", "t": "et", "g": "eg"}
+
+
+def ap(T, a):
+    if a[0] == "3":
+        return T[a[1]][:, :, a[3]:a[4]]
+    if a[0] == "k":
+        return T[a[1]][:, a[3], a[4]:a[5]]
+    if a[0] == "i":
+        return ap(T, a[1]).indirect(ap(T, a[2]))
+    if len(a) == 4:
+        return T[a[0]][:, a[1]:a[2]:a[3]]
+    return T[a[0]][:, a[1]:a[2]]
+
+
+def regs(a):
+    if a[0] == "3":
+        return [(a[1], k * a[2] + a[3], k * a[2] + a[4]) for k in range(8)]
+    if a[0] == "k":
+        return [(a[1], a[3] * a[2] + a[4], a[3] * a[2] + a[5])]
+    if a[0] == "i":
+        return regs(a[1])
+    return [(a[0], a[1], a[2])]
+
+
+def cnt(a):
+    if a[0] == "3":
+        return 8 * (a[4] - a[3])
+    if a[0] == "k":
+        return a[5] - a[4]
+    if a[0] == "i":
+        return 16 * cnt(a[2])
+    return len(range(a[1], a[2], a[3] if len(a) == 4 else 1))
+
+
+def psum(a):
+    return a[0][:2] == "pb"
+
+
+def wide(a):
+    return SCRATCH[regs(a)[0][0]][2] in (f32, i32)
+
+
+def program():
+    ops = []
+    ph = [-1.0]
+
+    def add(eng, fn, outs, ins, cost, kind="c", sem=None, nbytes=0, after=None):
+        rd, wr = [], []
+        for a in ins:
+            rd += regs(a)
+            if a[0] == "i":
+                rd += regs(a[2])
+        for a in outs:
+            wr += regs(a)
+            if a[0] == "i":
+                rd += regs(a[2])
+        ops.append({"eng": eng, "fn": fn, "rd": rd, "wr": wr, "cost": cost, "kind": kind, "sem": sem, "bytes": nbytes,
+                    "after": after, "ph": ph[0], "banks": sorted(set(r[0] for r in rd + wr if r[0][:2] == "pb"))})
+        z = (wr + rd)[0]
+        nm = {"pb1": "pb0", "pb3": "pb2"}.get(z[0], z[0].split("_")[0])
+        ops[-1]["cls"] = "%s:%s" % (eng, nm) + (":%d" % (z[1] // 192) if nm in ("pb0", "pb4", "pb6", "pb7") else "")
+        return len(ops) - 1
+
+    def vcost(o, i, two):
+        if o[0] == "i":
+            return 50 + SCAT * CY * cnt(o)
+        if i[0] == "i":
+            return 50 + GATH * CY * cnt(i)
+        return max(64, cnt(o) * (2 if two else 1)) * CY
+
+    def tt(o, a, b, op):
+        add("v", lambda q, T, X: q.tensor_tensor(ap(T, o), ap(T, a), ap(T, b), op), [o], [a, b],
+            vcost(o, a, not (psum(a) or psum(b))))
+
+    def ts(o, a, s1, s2, op0, op1=None):
+        ins = [a] + [z for z in (s1, s2) if isinstance(z, tuple)]
+
+        def fn(q, T, X):
+            z1 = ap(T, s1) if isinstance(s1, tuple) else s1
+            if op1 is None:
+                return q.tensor_scalar(ap(T, o), ap(T, a), z1, None, op0)
+            return q.tensor_scalar(ap(T, o), ap(T, a), z1, s2, op0, op1)
+        add("v", fn, [o], ins, vcost(o, a, False))
+
+    def cp(o, a):
+        add("v", lambda q, T, X: q.tensor_copy(ap(T, o), ap(T, a)), [o], [a], vcost(o, a, False))
+
+    def ms(o, c):
+        add("v", lambda q, T, X: q.memset(ap(T, o), c), [o], [], vcost(o, o, False))
+
+    def act(o, a, func, bias=None, scale=None):
+        def fn(q, T, X):
+            if bias is not None:
+                return q.activation(ap(T, o), ap(T, a), func, bias=bias)
+            if scale is not None:
+                return q.activation(ap(T, o), ap(T, a), func, scale=scale)
+            return q.activation(ap(T, o), ap(T, a), func)
+        add("s", fn, [o], [a], 65 + GATH * CY * cnt(a) if a[0] == "i" else max(64, cnt(o)) * CY)
+
+    def mm(items):
+        def fn(q, T, X):
+            for o, l, r, st, sp in items:
+                last = q.matmul(ap(T, o), ap(T, l), ap(T, r), st, sp)
+            return last
+        add("t", fn, [z[0] for z in items], [z[1] for z in items] + [z[2] for z in items],
+            sum(max(64, cnt(z[2])) * (4 if wide(z[2]) else 1) * PCY for z in items))
+
+    def iota(o, pat, base, cm):
+        def fn(q, T, X):
+            if SCRATCH[o[0]][2] == i32:
+                return q.iota(ap(T, o), pat, base, cm)
+            return q.iota(ap(T, o), pat, base, cm, allow_small_or_imprecise_dtypes=True)
+        add("g", fn, [o], [], 130 + 2 * CY * cnt(o))
+
+    def sel(o, a, pat, op, base, cm):
+        add("g", lambda q, T, X: q.affine_select(ap(T, o), ap(T, a), pat, op, 0.0, base, cm), [o], [a], 170 + 2 * CY * cnt(o))
+
+    def load(eng, o, name, lo, hi, sem, size):
+        add(eng, lambda q, T, X: q.dma_start(ap(T, o), T[name][:, lo:hi]), [o], [], 60, "dma", sem, 128 * (hi - lo) * size)
+
+    def store(eng, name, lo, hi, a):
+        add(eng, lambda q, T, X: q.dma_start(T[name][:, lo:hi], ap(T, a)), [], [a], 60, "dma", "out", 128 * (hi - lo) * 4)
+
+    ID, NID = ("idf", 0, 128), ("nidf", 0, 128)
+    load("y", ("rb", 0, 2048), "r0", 0, 2048, "l_rb", 2)
+    load("s", ("3", "dli", 24, 0, 24), "dl", 0, 192, "l_dl", 4)
+    load("s", ("nti", 0, 120), "nt", 0, 120, "l_nt", 4)
+    load("s", ("qui", 0, 72), "qu", 0, 72, "l_qu", 4)
+    for i in range(4):
+        load("y", ("wb", 768 * i, 768 * i + 768), "w0", 768 * i, 768 * i + 768, "l_w%d" % i, 2)
+    load("y", ("db", 0, 384), "d0", 0, 384, "l_d0", 2)
+    load("y", ("db", 384, 1920), "d0", 384, 1920, "l_d1", 2)
+    iota(("pj", 0, 1), [[0, 1]], 0, 1)
+    iota(("lb", 0, 12), [[0, 4], [4, 3]], 0, 0)
+    iota(("ld", 0, 12), [[24, 2], [0, 6]], 0, 0)
+    ts(("pk", 0, 1), ("pj", 0, 1), 15, None, A.bitwise_and)
+    cp(("jf", 0, 1), ("pk", 0, 1))
+    JF = ("jf", 0, 1)
+    ts(("lb", 0, 12), ("lb", 0, 12), JF, None, A.add)
+    ts(("lc", 0, 12), ("lb", 0, 12), 12.0, -12.0, A.is_ge, A.mult)
+    tt(("lb", 0, 12), ("lb", 0, 12), ("lc", 0, 12), A.add)
+    tt(("lb", 0, 12), ("lb", 0, 12), ("ld", 0, 12), A.add)
+    cp(("ll_0", 0, 12), ("lb", 0, 12))
+    ts(("ll_1", 0, 12), ("lb", 0, 12), 12.0, None, A.add)
+    ph[0] = 1.0
+    ms(("ones", 0, 128), 1.0)
+    sel(ID, ("ones", 0, 128), [[-1, 128]], A.is_equal, 0, 1)
+    ts(NID, ID, -1.0, None, A.mult)
+    cp(("idb", 0, 128), ID)
+    cp(("idf", 128, 256), ID)
+    ts(("i64", 0, 128), ID, 0.015625, None, A.mult)
+    ts(("idn", 0, 128), ID, -768.0, None, A.mult)
+    ms(("t8a", 0, 8), 16384.0)
+    ms(("z2", 0, 144), 0.0)
+    sel(("t8b", 0, 8), ("t8a", 0, 8), [[-16, 8]], A.is_ge, 0, 1)
+    sel(("t8c", 0, 8), ("t8b", 0, 8), [[16, 8]], A.is_ge, 15, -1)
+    cp(("z2", 15, 143, 16), ("t8c", 0, 8))
+    iota(("e1", 0, 192), [[-2048, 8], [768, 2], [16, 12]], 14336, 0)
+    iota(("e2", 0, 192), [[192, 8], [0, 24]], 0, 0)
+    iota(("e3", 0, 192), [[0, 8], [-1, 2], [0, 12]], 1, 0)
+    iota(("offc", 0, 96), [[192, 8], [16, 12]], 0, 0)
+    tt(("e2", 0, 192), ("e2", 0, 192), ("e3", 0, 192), A.mult)
+    tt(("e1", 0, 192), ("e1", 0, 192), ("e2", 0, 192), A.add)
+    ts(("ec", 0, 192), ("e1", 0, 192), JF, None, A.add)
+    ts(("offc", 0, 96), ("offc", 0, 96), JF, None, A.add)
+    if PE_MOD:
+        ts(("idk", 0, 128), ID, -1024.0, None, A.mult)
+        ms(("kil", 0, 96), 1024.0)
+    if S_SCAT:
+        iota(("za", 0, 256), [[1, 256]], -128, 0)
+        ts(("za", 0, 256), ("za", 0, 256), 2.0 ** -23, -9215827 * 2.0 ** -23, A.mult, A.add)
+        act(("zb", 0, 256), ("za", 0, 256), F.Sigmoid)
+        ops[-1]["cost"] += 1300
+        ts(("zb", 0, 256), ("zb", 0, 256), 0.25, None, A.is_equal)
+        tt(("zb", 0, 256), ("zb", 0, 256), ("za", 0, 256), A.mult)
+        add("v", lambda q, T, X: q.tensor_reduce(T.jf[:, 1:2], T.zb[:, :], AxisListType.X, A.min), [("jf", 1, 2)], [("zb", 0, 256)], 256 * CY)
+        ms(("quart", 0, 192), 1.0)
+        ts(("quart", 0, 192), ("quart", 0, 192), ("jf", 1, 2), None, A.mult)
+    else:
+        ms(("quart", 0, 192), 0.25)
+
+    def renew(n):
+        cp(("wo" + n, 0, 12), ("gg" + n, 0, 12))
+        o = ("i", ("w" + n, 0, 1728), ("wo" + n, 0, 12))
+        if S_SCAT:
+            act(o, ("quart", 0, NB), F.Sigmoid)
+            ops[-1]["cost"] = 65 + SCAT * CY * NB
+            ops[-1]["cls"] = "s:renew"
+        else:
+            cp(o, ("quart", 0, NB))
+
+    for h in range(H):
+        ms(("w_%d" % h, 1536, 1728), 0.0)
+    add("g", lambda q, T, X: q.dma_start(T.rr[:, :], T.r0[:, :]), [("rr", 0, 2048)], [("wb", 2304, 3072)], 1000, "dma", "l_rr", 128 * 2048 * 4)
+    ph[0] = -1.0
+    cp(("cd", 0, 24), ("nti", 0, 24))
+    cp(("cd", 24, 48), ("qui", 0, 24))
+    ts(("3", "vall", 144, 0, 24), ("3", "dli", 24, 0, 24), -1.0, None, A.mult)
+    ph[0] = 1.0
+    cp(("qa", 0, 72), ("qui", 0, 72))
+    cp(("ntu", 0, 120), ("nti", 0, 120))
+
+    def heads(s):
+        o = (s + 1) * 48
+        if s == S - 1:
+            cp(("cd", o, o + 24), ("qa", s * 24, s * 24 + 24))
+            return
+        tt(("cd", o, o + 24), ("nti", s * 24 + 24, s * 24 + 48), ("qa", s * 24, s * 24 + 24), A.subtract)
+        tt(("cd", o + 24, o + 48), ("qa", s * 24 + 24, s * 24 + 48), ("qa", s * 24, s * 24 + 24), A.subtract)
+
+    def tails(s0, s1):
+        o = ("pb4", 384, 384 + 24 * (s1 - s0))
+        it = [(o, ID, ("qa", s0 * 24, s1 * 24), True, False)]
+        it += [(o, NID, ("k", "xall", 120, k, s0 * 24, s1 * 24), False, False) for k in range(8)]
+        it += [(o, ID, ("k", "vall", 144, k, s0 * 24 + 24, s1 * 24 + 24), False, k == 7) for k in range(8)]
+        for a, b in ((0, 5), (5, 9), (9, 13), (13, 17)):
+            mm(it[a:b])
+        act(("qa", s0 * 24 + 72, s1 * 24 + 72), o, F.Copy)
+
+    def post(s, h):
+        n = "_%d" % h
+        v = ("3", "vall", 144, (s + 1) * 24 + 12 * h, (s + 1) * 24 + 12 * h + 12)
+        o = (s + 1) * 48
+        cb, xp = ("pb6", 192, 288), ("pb6", 288 + 96 * h, 384 + 96 * h)
+        if s == S - 1:
+            act(("bc" + n, 0, 96), ("i", ("cd", o, o + 24), ("ll" + n, 0, 6)), F.Copy)
+            act(cb, ("bc" + n, 0, 96), F.Copy)
+            tt(("3", "yds", 24, 12 * h, 12 * h + 12), cb, v, A.subtract)
+            return
+        act(("bc" + n, 0, 192), ("i", ("cd", o, o + 48), ("ll" + n, 0, 12)), F.Copy)
+        if PE_MOD and s >= 0:
+            mm([(cb, ID, ("bc" + n, 0, 96), True, False), (cb, ID, v, False, False)])
+            ops[-1]["wr"].append(("group6", 0, 1))
+            act(("su" + n, 0, 96), cb, F.Sign, bias=0.5)
+            mm([(cb, ("idk", 0, 128), ("su" + n, 0, 96), False, False), (cb, ("idb", 0, 128), ("kil", 0, 96), False, True)])
+            ops[-1]["wr"].append(("group6", 0, 1))
+            ops[-1]["cls"] = "t:mod"
+            cp(("off" + n, 0, 96), cb)
+        else:
+            if s < 0:
+                cp(("nh" + n, 0, 96), ("3", "dli", 24, 12 * h, 12 * h + 12))
+                tt(("ui" + n, 0, 96), ("i", ("cd", 0, 24), ("ll" + n, 0, 6)), ("nh" + n, 0, 96), A.subtract)
+            else:
+                act(cb, ("bc" + n, 0, 96), F.Copy)
+                tt(("ui" + n, 0, 96), cb, v, A.add)
+            ts(("uj" + n, 0, 96), ("ui" + n, 0, 96), 2047, None, A.bitwise_and)
+            cp(("off" + n, 0, 96), ("uj" + n, 0, 96))
+        if PE_X:
+            mm([(xp, ID, ("bc" + n, 96, 192), True, False), (xp, ID, v, False, True)])
+            ops[-1]["wr"].append(("group6", 0, 1))
+            ops[-1]["cls"] = "t:x"
+        else:
+            act(xp, ("bc" + n, 96, 192), F.Copy)
+            tt(xp, xp, v, A.add)
+        act(("aa" + n, 0, 96), xp, F.Abs)
+        act(("3", "xall", 120, (s + 1) * 24 + 12 * h, (s + 1) * 24 + 12 * h + 12), xp, F.Copy)
+        act(("ab" + n, 0, 96), ("aa" + n, 0, 96), F.Abs, bias=-1024.0)
+        act(("sg" + n, 0, 96), ("ab" + n, 0, 96), F.Sign, bias=-511.5)
+
+    ring = [0, 0]
+
+    def front(s, h):
+        n = "_%d" % h
+        y = ("pb7", 0, NB)
+        ph[0] = 6 * s + 3 * h
+        win = ("rb", 0, 2048) if s == 0 else ("rr", 0, 2048)
+        for i in range(4):
+            lo = 384 * i
+            xr = "pb%d" % (ring[0] % 2)
+            ring[0] += 1
+            if s == 0 and i in V_GATH[h]:
+                cp(("x" + n, lo, lo + 384), ("i", win, ("off" + n, 24 * i, 24 * i + 24)))
+            else:
+                act(("x" + n, lo, lo + 384), ("i", win, ("off" + n, 24 * i, 24 * i + 24)), F.Copy)
+            act((xr, 0, 384), ("x" + n, lo, lo + 384), F.Copy)
+            if s == 0:
+                for u in range(2):
+                    c0 = (2 * i + u) * 384 + NB * h
+                    tt(("p" + n, lo + NB * u, lo + NB * u + NB), (xr, NB * u, NB * u + NB), ("wb", c0, c0 + NB), A.mult)
+            elif i == 3:
+                for u in range(2):
+                    tt(("p" + n, lo + NB * u, lo + NB * u + NB), (xr, NB * u, NB * u + NB), ("w" + n, lo + NB * u, lo + NB * u + NB), A.mult)
+            else:
+                tt(("p" + n, lo, lo + 384), (xr, 0, 384), ("w" + n, lo, lo + 384), A.mult)
+            it = [(y, NID, ("p" + n, lo, lo + NB), i == 0, False), (y, NID, ("p" + n, lo + NB, lo + 384), False, False)]
+            if i == 3:
+                c0 = s * 384 + NB * h
+                mm(it[:1])
+                it = [it[1], (y, ("idb", 0, 128), ("db", c0, c0 + NB), False, True)]
+            mm(it)
+        es, ep = ("es" + n, 0, NB), ("pb4", NB * h, NB * h + NB)
+        if E_PSUM:
+            ts(ep, y, -2.0, 2.0, A.max, A.min)
+            ops[-1]["cls"] = "v:es"
+            act(es, ep, F.Copy)
+        else:
+            ts(es, y, -2.0, 2.0, A.max, A.min)
+            act(ep, es, F.Copy)
+        r = 16 * (1 + s)
+        c0 = s * 384 + NB * h
+        for u in range(2):
+            mm([(("pb%d" % u, 384, 480), ("idf", 128 - r, 256 - r), ("es" + n, 96 * u, 96 * u + 96), True, True)])
+            act(("snd", c0 + 96 * u, c0 + 96 * u + 96), ("pb%d" % u, 384, 480), F.Copy)
+
+        def send(q, T, X):
+            core, rank, topo = X
+            tr = []
+            for u in range(2):
+                b = 2 * h + u
+                dst = T.cores[(rank + 1 + b) % len(T.cores)]
+                rid, pid, _ = topo.addr(dst)
+                eng = topo.engines(core, dst)
+                half = len(eng) // 2
+                mask = sum(1 << e for e in eng[u * half:(u + 1) * half])
+                c = s * 384 + 96 * b
+                tr.append(RemoteDMATransfer(dst_ids=[DstId(rid=rid, pnc=pid)], dma_engine_mask=mask,
+                                            remote_sem=T.sem["arr%d_%d" % (s, h)], src=T.snd[:, c:c + 96], dst=T.land[:, c:c + 96]))
+            return q.remote_dma_fused(tr, local_sem=T.sem.sent)
+        k = add("g", send, [], [("snd", c0, c0 + NB)], 300, "send")
+        add(None, None, [("land", c0, c0 + NB)], [], 3500, "recv", "arr%d_%d" % (s, h), after=k)
+
+    def rest(s, h):
+        n = "_%d" % h
+        y = ("pb4", NB * h, NB * h + NB)
+        m0 = ("pb7", NB, 2 * NB)
+        ph[0] = 6 * s + 2 + 3 * h
+        far = DMA_UPD if s else ()
+        for i in far:
+            lo = 384 * i
+            tch, wch = ("t" + n, lo, lo + 384), ("w" + n, lo, lo + 384)
+            for u in range(2):
+                tt(("t" + n, lo + NB * u, lo + NB * u + NB), y, ("x" + n, lo + NB * u, lo + NB * u + NB), A.mult)
+            act(tch, tch, F.Copy, scale=0.015625)
+            add("g", lambda q, T, X, a=wch, b=tch: q.dma_start(ap(T, a), ap(T, b), accum_op=A.add), [wch], [wch, tch], GDMA,
+                "dma", "upd%d_%d_%d" % (s, h, i), 2 * 128 * 384 * 4)
+            act(("m" + n, lo, lo + 384), wch, F.Abs)
+            ops[-1]["cls"] = "s:far"
+        for i in range(4):
+            if i in far:
+                continue
+            lo = 384 * i
+            ur = "pb%d" % (2 + ring[1] % 2)
+            ring[1] += 1
+            for u in range(2):
+                tt(("t" + n, lo + NB * u, lo + NB * u + NB), y, ("x" + n, lo + NB * u, lo + NB * u + NB), A.mult)
+            tch, wch, mch = ("t" + n, lo, lo + 384), ("w" + n, lo, lo + 384), ("m" + n, lo, lo + 384)
+            wbs = [("wb", (2 * i + u) * 384 + NB * h, (2 * i + u) * 384 + NB * h + NB) for u in range(2)]
+            if i in PE_UPD:
+                if s == 0:
+                    mm([((ur, NB * u, NB * u + NB), ("idb", 0, 128), wbs[u], u == 0, False) for u in range(2)])
+                else:
+                    mm([((ur, 0, 384), ID, wch, True, False)])
+                ops[-1]["cls"] = "t:load"
+                mm([((ur, 0, 384), ("i64", 0, 128), tch, False, True)])
+                if i == 0:
+                    act(m0, (ur, 0, NB), F.Abs)
+                act(mch, (ur, 0, 384), F.Abs)
+                act(wch, (ur, 0, 384), F.Copy)
+            else:
+                act((ur, 0, 384), tch, F.Copy, scale=0.015625)
+                if s == 0:
+                    for u in range(2):
+                        tt(("w" + n, lo + NB * u, lo + NB * u + NB), (ur, NB * u, NB * u + NB), wbs[u], A.add)
+                else:
+                    tt(wch, (ur, 0, 384), wch, A.add)
+                if i == 0:
+                    act(m0, ("w" + n, 0, NB), F.Abs)
+                act(mch, wch, F.Abs)
+        acc = [("pb5", 0, NB), ("pb5", NB, 2 * NB)]
+        ph[0] = 6 * s + 2.2 + 3 * h
+        for k in range(1, 8):
+            for e in range(2):
+                tt(acc[e], m0 if k == 1 else acc[e], ("m" + n, NB * k, NB * k + NB), A.max if e else A.min)
+        ph[0] = 6 * s + 4 + 3 * h
+        for part in (1, 0):
+            for k in range(4 * part, 4 * part + 4):
+                for e in range(2):
+                    tt(("eq" + n, (2 * k + e) * NB, (2 * k + e + 1) * NB), acc[e], ("m" + n, NB * k, NB * k + NB), A.is_equal)
+            o = ("pb6", 96 * part, 96 * part + 96)
+            it = [(o, ID, ("ec", 96 * part, 96 * part + 96), True, False)]
+            it += [(("pb6", 24 * k + 12, 24 * k + 24), ("idn", 0, 128), ("sg" + n, 12 * k, 12 * k + 12), False, False)
+                   for k in range(4 * part, 4 * part + 4)]
+            mm(it)
+            ops[-1]["cls"] = "t:base"
+            ops[-1]["wr"].append(("group6", 0, 1))
+            mm([(o, ("z2", 15 - j, 143 - j), ("eq" + n, 1536 * part + j, 1536 * part + 1536, 16), False, j == 15) for j in range(16)])
+            ops[-1]["wr"].append(("group6", 0, 1))
+            if part:
+                act(("ssb" + n, 0, 96), o, F.Copy)
+        ph[0] = 6 * s + 5.1 + 3 * h
+        tt(("ta" + n, 0, 96), ("pb6", 0, 96), ("ssb" + n, 0, 96), A.max)
+        tt(("tb" + n, 0, 48), ("ta" + n, 0, 48), ("ta" + n, 48, 96), A.max)
+        tt(("tc" + n, 0, 24), ("tb" + n, 0, 24), ("tb" + n, 24, 48), A.max)
+        ts(("td" + n, 0, 24), ("tc" + n, 0, 24), 2047, None, A.bitwise_and)
+        tt(("gg" + n, 0, 12), ("td" + n, 0, 12), ("td" + n, 12, 24), A.max)
+        renew(n)
+        tt(("nh" + n, 0, 96), ("i", ("gg" + n, 0, 12), ("ll_0", 0, 6)), ("offc", 0, 96), A.not_equal)
+        tt(("3", "vall", 144, (s + 1) * 24 + 12 * h, (s + 1) * 24 + 12 * h + 12), ("pb6", 288 + 96 * h, 384 + 96 * h), ("nh" + n, 0, 96), A.mult)
+        post(s, h)
+
+    for h in range(H):
+        ph[0] = h - 1.0
+        post(-1, h)
+    ph[0] = 1.0
+    heads(0)
+    heads(1)
+    for s in range(S):
+        for h in range(H):
+            front(s, h)
+        if s == 2:
+            tails(0, 2)
+            heads(2)
+            heads(3)
+            heads(4)
+        if s == 4:
+            tails(2, 4)
+        for h in range(H):
+            c0 = s * 384 + NB * h
+            ph[0] = 6 * s + (5.3 if h else 4.5)
+            if s < S - 1:
+                cp(("i", ("rr", 0, 2048), ("ntu", s * 24 + 12 * h, s * 24 + 12 * h + 12)), ("land", c0, c0 + NB))
+        for h in range(H):
+            rest(s, h)
+            if s == S - 1:
+                for k in range(8):
+                    store("y" if h == 0 or k % 2 else "s", "yw", k * 384 + NB * h, k * 384 + NB * h + NB, ("w_%d" % h, NB * k, NB * k + NB))
+    store("y", "yr", 0, 384, ("land", 1536, 1920))
+    tails(4, 5)
+    store("y", "yd", 0, 192, ("3", "yds", 24, 0, 24))
+    store("s", "yq", 0, 72, ("qa", 120, 192))
+    return ops
+
+
+def edges(ops):
+    n = len(ops)
+    pred = [set() for _ in range(n)]
+    hist = {}
+    for i, o in enumerate(ops):
+        if o["after"] is not None:
+            pred[i].add(o["after"])
+        for rg, w in [(r, False) for r in o["rd"]] + [(r, True) for r in o["wr"]]:
+            for j, lo, hi, w2 in hist.get(rg[0], []):
+                if (w or w2) and lo < rg[2] and rg[1] < hi and j != i:
+                    pred[i].add(j)
+        for rg in o["wr"]:
+            hist[rg[0]] = [z for z in hist.get(rg[0], []) if not (rg[1] <= z[1] and z[2] <= rg[2])]
+        for rg, w in [(r, False) for r in o["rd"]] + [(r, True) for r in o["wr"]]:
+            hist.setdefault(rg[0], []).append((i, rg[1], rg[2], w))
+    succ = [[] for _ in range(n)]
+    for i in range(n):
+        for j in pred[i]:
+            succ[j].append(i)
+    return pred, succ
+
+
+def schedule(ops, data):
+    n = len(ops)
+    pred, succ = [set(p) for p in data[0]], data[1]
+    dur = [o["cost"] + (2000 + o["bytes"] / 180.0 if o["kind"] == "dma" else 0) for o in ops]
+    due, t = [0.0] * n, 0.0
+    for i in sorted(range(n), key=lambda z: (ops[z]["ph"], z)):
+        due[i] = t if ops[i]["eng"] == "v" else 1e9
+        t += ops[i]["cost"] if ops[i]["eng"] == "v" else 0.0
+    for i in range(n - 1, -1, -1):
+        due[i] = min([due[i], t + 1e4 - dur[i]] + [due[j] - dur[i] - LAM for j in succ[i]])
+    prio = [LEAD.get(ops[i]["cls"], 0.0) - due[i] for i in range(n)]
+    left = [len(p) for p in pred]
+    ready = [i for i in range(n) if left[i] == 0]
+    free = {"v": 0.0, "s": 0.0, "t": 0.0, "g": 0.0, "y": 0.0, None: 0.0}
+    fin, start, base = [0.0] * n, [0.0] * n, [0.0] * n
+    bank, order, wire = {}, [], 0.0
+    while ready:
+        can = []
+        for i in ready:
+            o = ops[i]
+            t = max(free[o["eng"]], base[i])
+            for b in o["banks"]:
+                for e, j in bank.get(b, {}).items():
+                    if e != o["eng"]:
+                        t = max(t, fin[j] + LAM)
+            can.append((t, i))
+        t0, i0 = min(can)
+        e0 = ops[i0]["eng"]
+        _, i, t = min((-prio[i], i, t) for t, i in can if ops[i]["eng"] == e0 and t <= t0 + LOOK.get(e0, 0.0))
+        o = ops[i]
+        ready.remove(i)
+        for b in o["banks"]:
+            for e, j in bank.setdefault(b, {}).items():
+                if e != o["eng"]:
+                    pred[i].add(j)
+            bank[b][o["eng"]] = i
+        start[i] = t
+        fin[i] = t + o["cost"]
+        if o["eng"] is not None:
+            free[o["eng"]] = fin[i]
+        if o["kind"] == "dma":
+            if o["bytes"] > 98000 and o["sem"] != "l_dl":
+                wire = max(wire, fin[i]) + o["bytes"] / 180.0
+                fin[i] = wire + 2000
+            else:
+                fin[i] += 2000 + o["bytes"] / 180.0
+        order.append(i)
+        for j in succ[i]:
+            both_pe = o["eng"] == "t" and ops[j]["eng"] == "t"
+            base[j] = max(base[j], fin[i] + (0.0 if both_pe else LAM))
+            left[j] -= 1
+            if left[j] == 0:
+                ready.append(j)
+    return order, pred, start, fin
+
+
+def waits(ops, order, pred):
+    seq, known, clock, need, raised = {}, {e: {} for e in "vstgy"}, {}, {}, set()
+    at = {}
+    for i in order:
+        o = ops[i]
+        e = o["eng"]
+        if o["kind"] == "recv":
+            clock[i] = {}
+            at[i] = (o["sem"], 1)
+            continue
+        kn = known[e]
+        lst = []
+        for j in sorted(pred[i], key=lambda z: -at[z][1]):
+            if e == "t" and ops[j]["eng"] == "t":
+                continue
+            key, val = at[j]
+            if kn.get(key, 0) >= val:
+                continue
+            lst.append(j)
+            kn[key] = val
+            if TRANS:
+                for k2, v2 in clock[j].items():
+                    if kn.get(k2, 0) < v2:
+                        kn[k2] = v2
+        need[i] = lst
+        raised.update(lst)
+        clock[i] = dict(kn)
+        if o["kind"] == "c":
+            seq[e] = seq.get(e, 0) + 1
+            at[i] = (e, seq[e])
+        else:
+            at[i] = ("op%d" % i, 1)
+    count, val = {}, {}
+    for i in order:
+        o = ops[i]
+        if o["kind"] == "c" and i in raised:
+            count[o["eng"]] = count.get(o["eng"], 0) + 1
+            val[i] = (ESEM[o["eng"]], count[o["eng"]])
+        elif o["kind"] in ("dma", "recv"):
+            val[i] = (o["sem"], 16)
+    return need, val
+
+
+PLAN = {}
+
+
+def plan():
+    if not PLAN:
+        ops = program()
+        order, pred, start, fin = schedule(ops, edges(ops))
+        need, val = waits(ops, order, pred)
+        PLAN.update(ops=ops, order=order, need=need, val=val, start=start, fin=fin, pred=pred)
+    return PLAN
+
+
+def rank_program(g, core, T, topo):
+    rank = T.rank_of(core)
+    if rank is None:
+        return
+    P = plan()
+    ops, need, val = P["ops"], P["need"], P["val"]
+    Q = {"v": g.vector, "s": g.scalar, "t": g.tensor, "g": g, "y": g.sync}
+    X = (core, rank, topo)
+    stores = sends = 0
+    for i in P["order"]:
+        o = ops[i]
+        if o["kind"] == "recv":
+            continue
+        q = Q[o["eng"]]
+        for j in need[i]:
+            q.wait_ge(T.sem[val[j][0]], val[j][1])
+        ins = o["fn"](q, T, X)
+        if o["kind"] == "dma":
+            ins.then_inc(T.sem[o["sem"]], 16)
+            stores += o["sem"] == "out"
+        elif o["kind"] == "send":
+            sends += 1
+        elif i in val:
+            ins.then_inc(T.sem[val[i][0]], 1)
+    g.wait_ge(T.sem.sent, 16 * sends)
+    g.wait_ge(T.sem.out, 16 * int(stores))

@@ -1,58 +1,95 @@
 from concourse.bass import DstId, RemoteDMATransfer
 from concourse.mybir import AluOpType as A, ActivationFunctionType as F, AxisListType
 
-S, H, NB = 5, 2, 192
-PE_UPD = (2, 3)
-DMA_UPD = ()
-GDMA = 1000.0
-S_SCAT = True
-PE_MOD = False
-PE_X = True
-E_PSUM = False
-V_GATH = ((1, 3), (1,))
-TRANS = True
-CY, PCY, LAM = 1.0, 0.5, 170.0
-GATH, SCAT = 1.55, 3.8
-LOOK = {"v": 150.0, "s": 150.0, "t": 600.0}
-LEAD = {'y:w': 13300, 's:snd': -16800, 's:bc': -19000, 'v:p': 1200, 'v:vall': 4400, 's:ssb': -34300, 's:m': 2700, 's:pb4:0': 1500, 's:pb7:1': 7700, 't:pb2': 12800, 't:pb4:2': -21100, 's:sg': -9800, 'v:w': 4500, 's:pb6:1': -17700, 's:x': -2900, 't:x': -10200, 'v:es': -500, 'v:rr': -1800, 'v:pb5': -1900, 's:aa': 7900, 'v:tc': 11100, 't:pb0:2': 3600, 'v:gg': -1400, 'v:ui': 19700, 's:pb0:0': 23400, 'v:td': 10900, 's:ab': 53700, 'v:nh': 26600, 's:w': -14500, 's:pb4:1': 28600, 'v:yds': -5000, 'v:tb': 14300, 'v:ta': 3800, 'v:off': 9600, 's:pb2': 3800, 's:qa': -4100, 't:pb6:0': -9900, 'v:cd': -6200, 't:base': -14500, 's:renew': -21900, 't:load': 1300, 's:xall': -5900, 'v:uj': 11600, 'v:eq': 200, 'v:x': 23000, 't:pb7:0': 1800, 'v:t': -900, 'v:wo': 5800, 'g:t8c': 1400, 'v:quart': -800, 'g:snd': 1000, 'v:t8a': -4000, 'g:offc': -9300, 'v:nidf': -6300, 'g:e2': -2100, 'y:yds': 1500, 'v:ec': -1400, 'v:idb': 3000, 'v:z2': -300, 's:zb': -1300, 'g:za': -600, 'y:land': 10300, 'g:t8b': -7100, 'v:e1': 1200, 'v:ones': 9300, 'v:za': -600, 'v:offc': 4700, 'v:jf': 3300, 'None:land': 2800, 'g:rr': 11600, 'v:idf': -2700, 'v:zb': 3400, 'v:qa': -1500, 'v:i64': -2500, 'g:e1': -5800, 'g:e3': -300, 'v:e2': 1300}
+S, H = 5, 3
+NB = 384 // H
+LC = NB // 16
+WP, LW = 8 * NB, 8 * LC
+TIE = 2048 if 9 * NB > 1024 else 1024
+BW = 512
+NBK = WP // BW
+CFG = {
+    "gb": tuple(range(0, WP + 1, 512)),
+    "pb": tuple(range(0, WP + 1, 512)),
+    "ub": (0, 512, 1024, 1152, 1536) if H == 2 else (0, 512, 768, 1024), "um": "TTTV" if H == 2 else "TTV",
+    "ab": tuple(range(0, WP + 1, 512)),
+    "vg": (0, 2, 4),
+    "erep": 2, "e_by": "t", "lanes": 2, "rep": 2, "e_at": "py", "mod": False, "base": False, "x_by": "t", "first": 0, "fix": True,
+    "v_gath": ((1,), (1,), (), ()),
+    "send": (0, 2, 4) if H == 2 else (0, 0, 2, 4), "direct": (0, 0, 0, 0), "rr": 1.0,
+    "cy": 0.83, "lam": 200.0, "ovh": 20.0, "tovh": 0.0, "wl": False, "gath": 1.55, "scat": 3.8, "rem": 5000.0,
+    "look": {"v": 0.0, "s": 0.0, "t": 0.0},
+    "win": {"v": 2.0}, "step": 18.0,
+    "shift": {"front": [0.0, 9.0], "update": [4.0, 13.0], "minmax": [6.0, 15.0], "masks": [8.2, 17.2],
+              "lists": [13.5, 22.5], "scatter": [13.0, 17.0], "tails": [8.0, 0], "front0": [0, -4.0]} if H == 2 else
+             {"front": [-0.5, 3.8, 8.0], "update": [3.0, 8.3, 14.1], "minmax": [6.5, 11.6, 17.6], "masks": [7.9, 14.1, 20.1],
+              "lists": [12.3, 17.2, 22.9], "scatter": [15.2, 12.4, 18.3], "tails": [10.9, 5.2, 2.4], "front0": [-0.7, -3.3, -3.9]},
+    "round": {
+        "front": 0.0, "front s:st": -1.5, "front s:x": -2.0, "front v:snd": 2.6, "front t:py": 0.3,
+        "update": 0.0, "update s:m0": 1.0, "update s:m": 1.1, "update s:w": 5.0, "update t:up": 0.5, "update t:load": -1.0,
+        "update t:e": -1.0, "update s:e": -1.0, "update s:up": 1.0, "update v:w": 1.3,
+        "minmax": 0.0, "minmax s:pl": 0.0, "masks": 0.0, "masks t:pv": 1.5, "masks s:ssb": 2.0,
+        "lists": 0.0, "lists s:w": 1.5, "lists s:bc": -2.0, "lists s:pv": -1.0, "lists t:pv": 2.5,
+        "lists s:aa": 4.0, "lists s:ab": 4.2, "lists s:sg": 4.4, "lists v:tb": 0.25, "lists v:tc": 0.5, "lists v:td": 0.75,
+        "lists v:gg": 1.0, "lists v:wo": 1.25, "lists v:nh": 1.3, "lists v:vall": 1.65, "lists v:ui": 1.9, "lists v:uj": 2.15,
+        "lists v:off": 2.4, "lists v:yds": 1.9, "scatter": 0.0, "tails": 0.0,
+    },
+    "pace": {"front v:p": 0.8, "front s:x": 0.8, "front s:st": 0.8, "front t:py": 0.8, "update v:t": 0.1, "minmax": 0.25, "masks v:eq": 0.5,
+             "masks t:pv": 1.4, "update s:m": 0.8, "update t:up": 0.8, "update s:w": 0.4},
+}
+
+CFG.update({'round': {'front': 0.1, 'front s:st': 1.6, 'front s:x': 1.6, 'front v:snd': 2.3, 'front t:py': 0.9, 'update': 0.6, 'update s:m0': 2.4, 'update s:m': 1.0, 'update s:w': 6.1, 'update t:up': 0.2, 'update t:load': 0.5, 'update t:e': -1.7, 'update s:e': -2.2, 'update s:up': 4.1, 'update v:w': 2.5, 'minmax': 0.0, 'minmax s:pl': -0.8, 'masks': 1.3, 'masks t:pv': 4.5, 'masks s:ssb': -7.2, 'lists': -0.4, 'lists s:w': 2.9, 'lists s:bc': -8.9, 'lists s:pv': 4.3, 'lists t:pv': 1.5, 'lists s:aa': -1.4, 'lists s:ab': 4.1, 'lists s:sg': 8.5, 'lists v:tb': -0.25, 'lists v:tc': 1.5, 'lists v:td': 1.25, 'lists v:gg': -0.3, 'lists v:wo': 1.45, 'lists v:nh': 1.6, 'lists v:vall': 2.25, 'lists v:ui': 2.2, 'lists v:uj': 3.35, 'lists v:off': 2.3, 'lists v:yds': 1.9, 'scatter': -2.7, 'tails': 0.2}, 'pace': {'front v:p': 2.25, 'front s:x': 2.025, 'front s:st': 0.95, 'front t:py': 1.19, 'update v:t': 0.045, 'minmax': 0.245, 'masks v:eq': 0.22, 'masks t:pv': 0.275, 'update s:m': 2.315, 'update t:up': 1.05, 'update s:w': 1.135}, 'shift': {'front': [-0.2, 3.9, 8.4], 'update': [1.9, 7.9, 13.7], 'minmax': [6.9, 11.1, 18.6], 'masks': [8.4, 14.1, 19.9], 'lists': [12.8, 18.5, 22.0], 'scatter': [14.0, 17.4, 21.9], 'tails': [8.9, 7.2, 2.1], 'front0': [-2.5, -2.4, -3.4], 'update0': [2.4, 0.0, 0.6], 'minmax0': [-0.9, 0.8, 0.1], 'masks0': [-0.3, 0.5, 0.7], 'front4': [1.7, 0.2, -3.3], 'update4': [-0.2, -0.8, 1.8], 'minmax4': [-1.5, 0.5, 1.0], 'masks4': [-0.9, 2.0, 1.6], 'lists4': [4.3, 0.9, 1.4]}, 'ub': (0, 512, 1024), 'um': 'TV', 'e_by': 't', 'ovh': 0, 'm0': False, 'lam': 200, 'rem': 4000, 'vg': (0, 2, 4), 'win': {'v': 3, 's': 100}, 'look': {'v': 0, 's': 0, 't': 150}, 'fix': False, 'direct': (0, 0, 0, 0), 'gb': (0, 512, 1024), 'pb': (0, 512, 1024), 'v_gath': ((1,), (), (), ()), 'step': 18})
+
+CFG.update({'round': {'front': 0.1, 'front s:st': -0.4, 'front s:x': 3.4, 'front v:snd': 1.7, 'front t:py': 1.8, 'update': -0.4, 'update s:m0': 2.0, 'update s:m': 4.6, 'update s:w': 8.0, 'update t:up': 0.2, 'update t:load': -0.4, 'update t:e': -1.4, 'update s:up': 5.0, 'update v:w': 2.1, 'minmax': 0.0, 'masks': 1.3, 'masks t:pv': 6.4, 'lists': 1.3, 'lists s:w': 5.1, 'lists s:bc': -8.5, 'lists s:pv': 3.9, 'lists t:pv': 2.8, 'lists s:aa': -0.9, 'lists s:ab': 5.7, 'lists s:sg': 9.5, 'lists v:tc': 1.4, 'lists v:gg': -0.6, 'lists v:wo': 2.25, 'lists v:nh': 2.3, 'lists v:vall': 2.05, 'lists v:ui': 0.4, 'lists v:uj': 1.95, 'lists v:off': 1.9, 'lists v:yds': 1.1, 'scatter': -1.4, 'tails': 1.2, 'masks t:base': 1.5, 'lists v:pv': 5.7}, 'rep': 1, 'erep': 1, 'pace': {'front v:p': 2.325, 'front s:x': 2.175, 'front s:st': 0.26, 'front t:py': 0.785, 'update v:t': 0, 'minmax': 0.275, 'masks v:eq': 0.085, 'update s:m': 2.45, 'update t:up': 1.815, 'update s:w': 0.865}, 'shift': {'front': [0.4, 3.8, 8.0], 'update': [2.1, 7.6, 14.0], 'minmax': [7.1, 9.9, 17.8], 'masks': [8.4, 15.0, 19.6], 'lists': [13.8, 18.6, 22.4], 'scatter': [16.3, 17.3, 22.6], 'tails': [10.2, 6.2, 2.8], 'front0': [-1.0, -1.3, -3.0], 'update0': [2.6, -0.2, 1.2], 'minmax0': [-0.5, 4.4, 0.4], 'masks0': [0.1, -0.5, 0.3], 'front4': [-1.0, -0.1, -3.2], 'update4': [1.3, -3.7, 0.8], 'minmax4': [-4.2, -2.4, -0.4], 'masks4': [-3.1, 0.7, 0.2], 'lists4': [2.3, 0.9, -0.5]}, 'base': True, 'x_by': 'v', 'e_at': 'pl', 'wl': True, 'win': {'v': 4, 's': 100}})
 
 f32, bf16, i32, u16 = "float32", "bfloat16", "int32", "uint16"
 SCRATCH = {
     "rb": ("sbuf", [128, 2048], bf16), "rr": ("sbuf", [128, 2048], f32), "wb": ("sbuf", [128, 3072], bf16),
     "db": ("sbuf", [128, 1920], bf16), "dli": ("sbuf", [128, 8, 24], i32), "nti": ("sbuf", [128, 120], i32),
     "qui": ("sbuf", [128, 72], i32), "ntu": ("sbuf", [128, 120], u16), "qa": ("sbuf", [128, 192], f32),
-    "cd": ("sbuf", [128, 288], f32), "vall": ("sbuf", [128, 8, 144], f32), "xall": ("sbuf", [128, 8, 120], f32),
+    "cd": ("sbuf", [128, 288], f32), "vall": ("sbuf", [128, 8, 144], f32), "gs": ("sbuf", [128, 144], f32),
     "yds": ("sbuf", [128, 8, 24], f32), "snd": ("sbuf", [128, 1920], f32), "land": ("sbuf", [128, 1920], f32),
-    "ones": ("sbuf", [128, 128], f32), "idf": ("sbuf", [128, 256], f32), "nidf": ("sbuf", [128, 128], f32),
-    "i64": ("sbuf", [128, 128], f32), "idb": ("sbuf", [128, 128], bf16), "idn": ("sbuf", [128, 128], bf16),
+    "ll": ("sbuf", [128, 24], u16), "e3": ("sbuf", [128, LW], f32), "idk": ("sbuf", [128, 128], bf16), "kil": ("sbuf", [128, LW], bf16),
+    "keep": ("sbuf", [128, 2 * LW], f32), "jg": ("sbuf", [128, 4], f32), "turn": ("sbuf", [128, 8], u16),
+    "ones": ("sbuf", [128, 256], f32), "idf": ("sbuf", [128, 256], f32), "nidf": ("sbuf", [128, 256], f32),
+    "i64": ("sbuf", [128, 128], f32), "idb": ("sbuf", [128, 256], bf16), "idn": ("sbuf", [128, 128], bf16),
+    "i8": ("sbuf", [128, 128], f32),
     "z2": ("sbuf", [128, 144], bf16), "t8a": ("sbuf", [128, 8], f32), "t8b": ("sbuf", [128, 8], f32),
     "t8c": ("sbuf", [128, 8], f32), "pj": ("sbuf", [128, 4], i32), "pk": ("sbuf", [128, 4], i32), "jf": ("sbuf", [128, 4], f32),
-    "e1": ("sbuf", [128, 192], f32), "e2": ("sbuf", [128, 192], f32), "e3": ("sbuf", [128, 192], f32),
-    "ec": ("sbuf", [128, 192], f32), "offc": ("sbuf", [128, 96], f32), "lb": ("sbuf", [128, 12], f32),
-    "lc": ("sbuf", [128, 12], f32), "ld": ("sbuf", [128, 12], f32), "quart": ("sbuf", [128, 192], f32),
-    "za": ("sbuf", [128, 256], f32), "zb": ("sbuf", [128, 256], f32), "idk": ("sbuf", [128, 128], bf16), "kil": ("sbuf", [128, 96], bf16),
+    "e1": ("sbuf", [128, LW], f32), "e2": ("sbuf", [128, 2 * LW], f32), "eca": ("sbuf", [128, 2 * LW], bf16),
+    "ecb": ("sbuf", [128, 2 * LW], bf16), "offc": ("sbuf", [128, LW], f32), "lb": ("sbuf", [128, 24], f32),
+    "lc": ("sbuf", [128, 24], i32), "ld": ("sbuf", [128, 24], f32), "le": ("sbuf", [128, 24], f32), "quart": ("sbuf", [128, 256], f32),
+    "za": ("sbuf", [128, 128], f32), "zb": ("sbuf", [128, 128], f32),
 }
 for _h in range(H):
-    for _n, _c, _d in (("w", 1728, f32), ("x", 1536, f32), ("p", 1536, f32), ("t", 1536, f32), ("m", 1536, f32),
-                       ("eq", 3072, bf16), ("es", 192, f32), ("off", 96, u16), ("ui", 96, i32), ("uj", 96, i32),
-                       ("ssb", 96, f32), ("ta", 96, f32), ("tb", 48, f32), ("tc", 24, i32), ("td", 24, i32),
-                       ("gg", 16, f32), ("wo", 12, u16), ("nh", 96, f32), ("bc", 192, f32), ("aa", 96, f32),
-                       ("ab", 96, f32), ("sg", 96, bf16), ("su", 96, bf16), ("ll", 12, u16)):
-        SCRATCH[_n + "_%d" % _h] = ("sbuf", [128, _c], _d)
-for _b in range(8):
-    SCRATCH["pb%d" % _b] = ("psum", [128, 512], f32)
+    for _n, _c, _d in (("w", [2 * WP], f32), ("x", [WP], f32), ("p", [WP], f32), ("t", [WP], f32), ("m", [WP], f32),
+                       ("eq", [2 * NB, 8], bf16), ("sb", [2 * NB], f32), ("off", [LW], u16), ("ui", [LW], i32), ("uj", [LW], i32),
+                       ("ssb", [LW], f32), ("ta", [2 * LW], f32), ("tb", [2, 2 * LC], f32), ("tc", [2 * LC], i32), ("td", [2 * LC], i32),
+                       ("gg", [16], i32), ("wo", [LC], u16), ("nh", [LW], f32), ("bc", [2 * LW], f32), ("aa", [LW], f32),
+                       ("ab", [LW], f32), ("sg", [LW], bf16), ("su", [LW], bf16)):
+        SCRATCH[_n + "_%d" % _h] = ("sbuf", [128] + _c, _d)
+for _b in ("st_0", "st_1", "up_0", "up_1", "py"):
+    SCRATCH[_b] = ("psum", [128, BW], f32)
+SCRATCH["pv"] = ("psum", [128, BW], f32)
+for _b in range(1 if H == 2 else 2):
+    SCRATCH["pl_%d" % _b] = ("psum", [128, 2, BW if H == 2 else BW // 2], f32)
 
-LOADS = ["l_rb", "l_dl", "l_nt", "l_qu", "l_w0", "l_w1", "l_w2", "l_w3", "l_d0", "l_d1", "l_rr"]
-SEMAPHORES = ["ev", "es", "et", "eg", "sent", "out"] + LOADS + ["arr%d_%d" % (s, h) for s in range(S) for h in range(H)]
-SEMAPHORES += ["upd%d_%d_%d" % (s, h, i) for s in range(1, S) for h in range(H) for i in DMA_UPD]
+LOADS = ["l_rb", "l_n0", "l_dl", "l_nt", "l_qu", "l_w0", "l_w1", "l_w2", "l_w3", "l_d0", "l_d1"]
+SEMAPHORES = ["ev", "es", "et", "eg", "sent", "out"] + LOADS + ["upd%d_%d" % (s, h) for s in range(1, S) for h in range(H)] + ["arr%d_%d" % (s, h) for s in range(S) for h in range(H)]
 ESEM = {"v": "ev", "s": "es", "t": "et", "g": "eg"}
 
 
 def ap(T, a):
     if a[0] == "3":
-        return T[a[1]][:, :, a[3]:a[4]]
+        return T[a[1]][:, :, a[2]:a[3]]
     if a[0] == "k":
-        return T[a[1]][:, a[3], a[4]:a[5]]
+        return T[a[1]][:, a[2], a[3]:a[4]]
+    if a[0] == "r":
+        return T[a[1]][:, a[2]:a[3], :]
+    if a[0] == "c":
+        return T[a[1]][:, a[2]:a[3], a[4]]
+    if a[0] == "j":
+        return T[a[1]][:, a[2]::16, :]
     if a[0] == "i":
         return ap(T, a[1]).indirect(ap(T, a[2]))
     if len(a) == 4:
@@ -62,37 +99,58 @@ def ap(T, a):
 
 def regs(a):
     if a[0] == "3":
-        return [(a[1], k * a[2] + a[3], k * a[2] + a[4]) for k in range(8)]
+        n, w = SCRATCH[a[1]][1][1:]
+        return [(a[1], k * w + a[2], k * w + a[3]) for k in range(n)]
     if a[0] == "k":
-        return [(a[1], a[3] * a[2] + a[4], a[3] * a[2] + a[5])]
+        w = SCRATCH[a[1]][1][2]
+        return [(a[1], a[2] * w + a[3], a[2] * w + a[4])]
+    if a[0] == "r":
+        w = SCRATCH[a[1]][1][2]
+        return [(a[1], a[2] * w, a[3] * w)]
+    if a[0] == "c":
+        return [(a[1], a[4] * 2 * NB + a[2], a[4] * 2 * NB + a[3])]
+    if a[0] == "j":
+        return [(a[1], 0, 2 * WP)]
     if a[0] == "i":
         return regs(a[1])
     return [(a[0], a[1], a[2])]
 
 
 def cnt(a):
-    if a[0] == "3":
-        return 8 * (a[4] - a[3])
-    if a[0] == "k":
-        return a[5] - a[4]
     if a[0] == "i":
         return 16 * cnt(a[2])
-    return len(range(a[1], a[2], a[3] if len(a) == 4 else 1))
+    if a[0] == "j":
+        return NB
+    if len(a) == 4 and a[0] in SCRATCH:
+        return len(range(a[1], a[2], a[3]))
+    return sum(z[2] - z[1] for z in regs(a))
 
 
 def psum(a):
-    return a[0][:2] == "pb"
+    return SCRATCH[regs(a)[0][0]][0] == "psum"
 
 
 def wide(a):
     return SCRATCH[regs(a)[0][0]][2] in (f32, i32)
 
 
-def program():
-    ops = []
-    ph = [-1.0]
+def part(a, lo, hi):
+    return a if a[0] == "r" else a[:-2] + (a[-2] + lo, a[-2] + hi)
 
-    def add(eng, fn, outs, ins, cost, kind="c", sem=None, nbytes=0, after=None):
+
+def pairs(b):
+    return list(zip(b[:-1], b[1:]))
+
+
+def program():
+    C = CFG
+    ops = []
+    tag = ["start", -1.0]
+
+    def phase(name, s, h):
+        tag[0] = "%s %d %d" % (name, s, h)
+
+    def add(eng, fn, outs, ins, cost, kind="c", sem=None, nbytes=0, after=None, ind=None, group=None, nins=1):
         rd, wr = [], []
         for a in ins:
             rd += regs(a)
@@ -102,379 +160,463 @@ def program():
             wr += regs(a)
             if a[0] == "i":
                 rd += regs(a[2])
-        ops.append({"eng": eng, "fn": fn, "rd": rd, "wr": wr, "cost": cost, "kind": kind, "sem": sem, "bytes": nbytes,
-                    "after": after, "ph": ph[0], "banks": sorted(set(r[0] for r in rd + wr if r[0][:2] == "pb"))})
-        z = (wr + rd)[0]
-        nm = {"pb1": "pb0", "pb3": "pb2"}.get(z[0], z[0].split("_")[0])
-        ops[-1]["cls"] = "%s:%s" % (eng, nm) + (":%d" % (z[1] // 192) if nm in ("pb0", "pb4", "pb6", "pb7") else "")
+        banks = sorted(set((r[0], r[1] // BW) for r in rd + wr if SCRATCH[r[0]][0] == "psum"))
+        ops.append({"group": group, "eng": eng, "fn": fn, "rd": rd, "wr": wr, "cost": cost, "kind": kind, "sem": sem, "bytes": nbytes,
+                    "after": after, "banks": banks, "ind": ind, "tag": tag[0], "ph": tag[1], "nins": nins,
+                    "cls": "%s:%s" % (eng, (wr + rd)[0][0].split("_")[0])})
         return len(ops) - 1
 
-    def vcost(o, i, two):
+    def vec(fn, o, ins, two=False):
         if o[0] == "i":
-            return 50 + SCAT * CY * cnt(o)
-        if i[0] == "i":
-            return 50 + GATH * CY * cnt(i)
-        return max(64, cnt(o) * (2 if two else 1)) * CY
+            add("v", fn, [o], ins, 60 + C["scat"] * cnt(o), ind="s")
+        elif ins and ins[0][0] == "i":
+            add("v", fn, [o], ins, 60 + C["gath"] * cnt(o), ind="g")
+        else:
+            half = not two and not wide(o) and not any(wide(a) for a in ins[:1])
+            add("v", fn, [o], ins, max(64, cnt(o) * (2 if two else 0.5 if half else 1)))
+            ops[-1]["raw"] = cnt(o) * (2 if two else 0.5 if half else 1)
 
     def tt(o, a, b, op):
-        add("v", lambda q, T, X: q.tensor_tensor(ap(T, o), ap(T, a), ap(T, b), op), [o], [a, b],
-            vcost(o, a, not (psum(a) or psum(b))))
+        vec(lambda q, T, X: q.tensor_tensor(ap(T, o), ap(T, a), ap(T, b), op), o, [a, b], not (psum(a) or psum(b)))
 
     def ts(o, a, s1, s2, op0, op1=None):
-        ins = [a] + [z for z in (s1, s2) if isinstance(z, tuple)]
-
         def fn(q, T, X):
             z1 = ap(T, s1) if isinstance(s1, tuple) else s1
             if op1 is None:
                 return q.tensor_scalar(ap(T, o), ap(T, a), z1, None, op0)
             return q.tensor_scalar(ap(T, o), ap(T, a), z1, s2, op0, op1)
-        add("v", fn, [o], ins, vcost(o, a, False))
+        vec(fn, o, [a] + [z for z in (s1, s2) if isinstance(z, tuple)])
 
     def cp(o, a):
-        add("v", lambda q, T, X: q.tensor_copy(ap(T, o), ap(T, a)), [o], [a], vcost(o, a, False))
+        vec(lambda q, T, X: q.tensor_copy(ap(T, o), ap(T, a)), o, [a])
 
     def ms(o, c):
-        add("v", lambda q, T, X: q.memset(ap(T, o), c), [o], [], vcost(o, o, False))
+        vec(lambda q, T, X: q.memset(ap(T, o), c), o, [])
 
     def act(o, a, func, bias=None, scale=None):
         def fn(q, T, X):
-            if bias is not None:
-                return q.activation(ap(T, o), ap(T, a), func, bias=bias)
             if scale is not None:
-                return q.activation(ap(T, o), ap(T, a), func, scale=scale)
+                return q.activation(ap(T, o), ap(T, a), func, scale=ap(T, scale) if isinstance(scale, tuple) else scale)
+            if bias is not None:
+                return q.activation(ap(T, o), ap(T, a), func, bias=ap(T, bias) if isinstance(bias, tuple) else bias)
             return q.activation(ap(T, o), ap(T, a), func)
-        add("s", fn, [o], [a], 65 + GATH * CY * cnt(a) if a[0] == "i" else max(64, cnt(o)) * CY)
+        if o[0] == "i":
+            add("s", fn, [o], [a], 78 + C["scat"] * cnt(o), ind="s")
+        elif a[0] == "i":
+            add("s", fn, [o], [a], 78 + C["gath"] * cnt(o), ind="g")
+        else:
+            add("s", fn, [o], [a] + [z for z in (bias, scale) if isinstance(z, tuple)], max(64, cnt(o)))
+            ops[-1]["raw"] = cnt(o)
 
-    def mm(items):
+    def scp(o, a):
+        act(o, a, F.Copy)
+
+    def mm(items, group=None):
         def fn(q, T, X):
             for o, l, r, st, sp in items:
                 last = q.matmul(ap(T, o), ap(T, l), ap(T, r), st, sp)
             return last
-        add("t", fn, [z[0] for z in items], [z[1] for z in items] + [z[2] for z in items],
-            sum(max(64, cnt(z[2])) * (4 if wide(z[2]) else 1) * PCY for z in items))
+        add("t", fn, [z[0] for z in items], [z[1] for z in items] + [z[2] for z in items] + [z[0] for z in items if not z[3]],
+            sum(max(64, cnt(z[2])) * (2 if wide(z[2]) else 0.5) for z in items),
+            group=(regs(items[0][0])[0][0], items[0][3], items[-1][4]), nins=len(items))
+        ops[-1]["raw"] = sum(cnt(z[2]) * (2 if wide(z[2]) else 0.5) for z in items)
 
     def iota(o, pat, base, cm):
         def fn(q, T, X):
             if SCRATCH[o[0]][2] == i32:
                 return q.iota(ap(T, o), pat, base, cm)
             return q.iota(ap(T, o), pat, base, cm, allow_small_or_imprecise_dtypes=True)
-        add("g", fn, [o], [], 130 + 2 * CY * cnt(o))
+        add("g", fn, [o], [], 160 + 2 * cnt(o))
 
     def sel(o, a, pat, op, base, cm):
-        add("g", lambda q, T, X: q.affine_select(ap(T, o), ap(T, a), pat, op, 0.0, base, cm), [o], [a], 170 + 2 * CY * cnt(o))
+        add("g", lambda q, T, X: q.affine_select(ap(T, o), ap(T, a), pat, op, 0.0, base, cm), [o], [a], 200 + 2 * cnt(o))
 
     def load(eng, o, name, lo, hi, sem, size):
-        add(eng, lambda q, T, X: q.dma_start(ap(T, o), T[name][:, lo:hi]), [o], [], 60, "dma", sem, 128 * (hi - lo) * size)
+        add(eng, lambda q, T, X: q.dma_start(ap(T, o), T[name][:, lo:hi]), [o], [], 70, "dma", sem, 128 * (hi - lo) * size)
 
     def store(eng, name, lo, hi, a):
-        add(eng, lambda q, T, X: q.dma_start(T[name][:, lo:hi], ap(T, a)), [], [a], 60, "dma", "out", 128 * (hi - lo) * 4)
+        add(eng, lambda q, T, X: q.dma_start(T[name][:, lo:hi], ap(T, a)), [], [a], 70, "dma", "out", 128 * (hi - lo) * 4)
 
-    ID, NID = ("idf", 0, 128), ("nidf", 0, 128)
+    ID, NID, IDB = ("idf", 0, 128), ("nidf", 0, 128), ("idb", 0, 128)
+    tag[1] = -3.0
+    load("s", ("3", "dli", 0, 24), "dl", 0, 192, "l_dl", 4)
+    load("y", ("nti", 0, 24), "nt", 0, 24, "l_n0", 4)
     load("y", ("rb", 0, 2048), "r0", 0, 2048, "l_rb", 2)
-    load("s", ("3", "dli", 24, 0, 24), "dl", 0, 192, "l_dl", 4)
-    load("s", ("nti", 0, 120), "nt", 0, 120, "l_nt", 4)
-    load("s", ("qui", 0, 72), "qu", 0, 72, "l_qu", 4)
-    for i in range(4):
-        load("y", ("wb", 768 * i, 768 * i + 768), "w0", 768 * i, 768 * i + 768, "l_w%d" % i, 2)
-    load("y", ("db", 0, 384), "d0", 0, 384, "l_d0", 2)
+    if C["wl"]:
+        for a, b, z in ((0, NB, 0), (NB, 384, 2)):
+            for k in range(8):
+                load("y" if k % 2 or z else "s", ("wb", 384 * k + a, 384 * k + b), "w0", 384 * k + a, 384 * k + b, "l_w%d" % (z + k // 4), 2)
+            if z == 0:
+                load("y", ("db", 0, 384), "d0", 0, 384, "l_d0", 2)
+                load("y", ("qui", 0, 72), "qu", 0, 72, "l_qu", 4)
+    else:
+        load("s", ("qui", 0, 72), "qu", 0, 72, "l_qu", 4)
+        for i in range(4):
+            load("y", ("wb", 768 * i, 768 * i + 768), "w0", 768 * i, 768 * i + 768, "l_w%d" % i, 2)
+        load("y", ("db", 0, 384), "d0", 0, 384, "l_d0", 2)
+    load("y", ("nti", 24, 120), "nt", 24, 120, "l_nt", 4)
     load("y", ("db", 384, 1920), "d0", 384, 1920, "l_d1", 2)
+    tag[1] = -2.0
     iota(("pj", 0, 1), [[0, 1]], 0, 1)
-    iota(("lb", 0, 12), [[0, 4], [4, 3]], 0, 0)
-    iota(("ld", 0, 12), [[24, 2], [0, 6]], 0, 0)
+    iota(("ld", 0, H * LC), [[LC, H], [24, 2], [0, LC // 2]], 0, 0)
     ts(("pk", 0, 1), ("pj", 0, 1), 15, None, A.bitwise_and)
-    cp(("jf", 0, 1), ("pk", 0, 1))
     JF = ("jf", 0, 1)
-    ts(("lb", 0, 12), ("lb", 0, 12), JF, None, A.add)
-    ts(("lc", 0, 12), ("lb", 0, 12), 12.0, -12.0, A.is_ge, A.mult)
-    tt(("lb", 0, 12), ("lb", 0, 12), ("lc", 0, 12), A.add)
-    tt(("lb", 0, 12), ("lb", 0, 12), ("ld", 0, 12), A.add)
-    cp(("ll_0", 0, 12), ("lb", 0, 12))
-    ts(("ll_1", 0, 12), ("lb", 0, 12), 12.0, None, A.add)
-    ph[0] = 1.0
-    ms(("ones", 0, 128), 1.0)
-    sel(ID, ("ones", 0, 128), [[-1, 128]], A.is_equal, 0, 1)
-    ts(NID, ID, -1.0, None, A.mult)
-    cp(("idb", 0, 128), ID)
-    cp(("idf", 128, 256), ID)
-    ts(("i64", 0, 128), ID, 0.015625, None, A.mult)
-    ts(("idn", 0, 128), ID, -768.0, None, A.mult)
-    ms(("t8a", 0, 8), 16384.0)
+    if LC == 8:
+        ts(("pk", 1, 2), ("pj", 0, 1), 7, None, A.bitwise_and)
+        cp(("jf", 0, 2), ("pk", 0, 2))
+        ts(("ll", 0, H * LC), ("ld", 0, H * LC), ("jf", 1, 2), None, A.add)
+    else:
+        cp(("jf", 0, 1), ("pk", 0, 1))
+        iota(("lb", 0, H * LC), [[0, H], [16, LC]], 0, 0)
+        ts(("lb", 0, H * LC), ("lb", 0, H * LC), JF, None, A.add)
+        ts(("lc", 0, H * LC), ("lb", 0, H * LC), 0.5 - LC / 2.0, 1.0 / LC, A.add, A.mult)
+        ts(("le", 0, H * LC), ("lc", 0, H * LC), -float(LC), None, A.mult)
+        tt(("lb", 0, H * LC), ("lb", 0, H * LC), ("ld", 0, H * LC), A.add)
+        tt(("lb", 0, H * LC), ("lb", 0, H * LC), ("le", 0, H * LC), A.add)
+        cp(("ll", 0, H * LC), ("lb", 0, H * LC))
+    tag[1] = -0.5
+    ms(("ones", 0, 256), 1.0)
+    sel(("idf", 0, 256), ("ones", 0, 256), [[0, 2], [-1, 128]], A.is_equal, 0, 1)
+    scp(("idb", 0, 256), ("idf", 0, 256))
+    act(("nidf", 0, 256), ("idf", 0, 256), F.Copy, scale=-1.0)
+    tag[1] = 0.1
+    act(("i64", 0, 128), ID, F.Copy, scale=0.015625)
+    act(("i8", 0, 128), ID, F.Copy, scale=-8.0)
+    act(("idn", 0, 128), ID, F.Copy, scale=-4.0 * NB)
+    if C["mod"]:
+        act(("idk", 0, 128), ID, F.Copy, scale=-1024.0)
+        ms(("kil", 0, LW), -1.0)
+    ms(("t8a", 0, 8), 8.0 * TIE)
     ms(("z2", 0, 144), 0.0)
     sel(("t8b", 0, 8), ("t8a", 0, 8), [[-16, 8]], A.is_ge, 0, 1)
     sel(("t8c", 0, 8), ("t8b", 0, 8), [[16, 8]], A.is_ge, 15, -1)
     cp(("z2", 15, 143, 16), ("t8c", 0, 8))
-    iota(("e1", 0, 192), [[-2048, 8], [768, 2], [16, 12]], 14336, 0)
-    iota(("e2", 0, 192), [[192, 8], [0, 24]], 0, 0)
-    iota(("e3", 0, 192), [[0, 8], [-1, 2], [0, 12]], 1, 0)
-    iota(("offc", 0, 96), [[192, 8], [16, 12]], 0, 0)
-    tt(("e2", 0, 192), ("e2", 0, 192), ("e3", 0, 192), A.mult)
-    tt(("e1", 0, 192), ("e1", 0, 192), ("e2", 0, 192), A.add)
-    ts(("ec", 0, 192), ("e1", 0, 192), JF, None, A.add)
-    ts(("offc", 0, 96), ("offc", 0, 96), JF, None, A.add)
-    if PE_MOD:
-        ts(("idk", 0, 128), ID, -1024.0, None, A.mult)
-        ms(("kil", 0, 96), 1024.0)
-    if S_SCAT:
-        iota(("za", 0, 256), [[1, 256]], -128, 0)
-        ts(("za", 0, 256), ("za", 0, 256), 2.0 ** -23, -9215827 * 2.0 ** -23, A.mult, A.add)
-        act(("zb", 0, 256), ("za", 0, 256), F.Sigmoid)
-        ops[-1]["cost"] += 1300
-        ts(("zb", 0, 256), ("zb", 0, 256), 0.25, None, A.is_equal)
-        tt(("zb", 0, 256), ("zb", 0, 256), ("za", 0, 256), A.mult)
-        add("v", lambda q, T, X: q.tensor_reduce(T.jf[:, 1:2], T.zb[:, :], AxisListType.X, A.min), [("jf", 1, 2)], [("zb", 0, 256)], 256 * CY)
-        ms(("quart", 0, 192), 1.0)
-        ts(("quart", 0, 192), ("quart", 0, 192), ("jf", 1, 2), None, A.mult)
-    else:
-        ms(("quart", 0, 192), 0.25)
-
-    def renew(n):
-        cp(("wo" + n, 0, 12), ("gg" + n, 0, 12))
-        o = ("i", ("w" + n, 0, 1728), ("wo" + n, 0, 12))
-        if S_SCAT:
-            act(o, ("quart", 0, NB), F.Sigmoid)
-            ops[-1]["cost"] = 65 + SCAT * CY * NB
-            ops[-1]["cls"] = "s:renew"
-        else:
-            cp(o, ("quart", 0, NB))
-
-    for h in range(H):
-        ms(("w_%d" % h, 1536, 1728), 0.0)
-    add("g", lambda q, T, X: q.dma_start(T.rr[:, :], T.r0[:, :]), [("rr", 0, 2048)], [("wb", 2304, 3072)], 1000, "dma", "l_rr", 128 * 2048 * 4)
-    ph[0] = -1.0
+    iota(("eca", 0, LW), [[0, LC], [NB - TIE, 8]], 7 * TIE, 0)
+    iota(("eca", LW, 2 * LW), [[0, LC], [-TIE, 8]], 7 * TIE + 4 * NB, 0)
+    sel(("keep", 0, 2 * LW), ("ones", 0, 2 * LW), [[0, 2 * LC], [1, 8]], A.is_gt, 0, 0)
+    iota(("e2", 0, LW), [[16, LC], [0, 8]], 0, 0)
+    act(("ecb", 0, LW), ("e2", 0, LW), F.Identity, bias=JF)
+    iota(("le", 0, LC // 2), [[2, LC // 2]], 0, 0)
+    ts(("pk", 2, 3), ("pj", 0, 1), 7, None, A.bitwise_and)
+    ts(("pk", 3, 4), ("pj", 0, 1), 3, 1, A.logical_shift_right, A.bitwise_and)
+    ts(("jg", 0, 1), ("pk", 2, 3), float(LC), None, A.mult)
+    tt(("jg", 1, 2), ("jg", 0, 1), ("pk", 3, 4), A.add)
+    ts(("turn", 0, LC // 2), ("le", 0, LC // 2), ("jg", 1, 2), None, A.add)
+    iota(("e3", 0, LW), [[NB, 8], [16, LC]], 0, 0)
+    act(("offc", 0, LW), ("e3", 0, LW), F.Identity, bias=JF)
+    tag[1] = -1.5
+    iota(("za", 0, 128), [[1, 128]], -9215827 - 64, 0)
+    act(("za", 0, 128), ("za", 0, 128), F.Copy, scale=2.0 ** -23)
+    act(("zb", 0, 128), ("za", 0, 128), F.Sigmoid)
+    ops[-1]["cost"] += 1570
+    ops[-1]["raw"] += 1570
+    tag[1] = 0.1
+    ts(("zb", 0, 128), ("zb", 0, 128), 0.25, None, A.is_equal)
+    tt(("zb", 0, 128), ("zb", 0, 128), ("za", 0, 128), A.mult)
+    add("v", lambda q, T, X: q.tensor_reduce(T.jf[:, 2:3], T.zb[:, :], AxisListType.X, A.min), [("jf", 2, 3)], [("zb", 0, 128)], 128)
+    act(("quart", 0, NB), ("ones", 0, NB), F.Copy, scale=("jf", 2, 3))
+    tag[1] = C["rr"]
+    for z in range(0, 2048, 1024):
+        scp(("rr", z, z + 1024), ("rb", z, z + 1024))
+    tag[1] = -1.0
     cp(("cd", 0, 24), ("nti", 0, 24))
+    tag[1] = 0.1
     cp(("cd", 24, 48), ("qui", 0, 24))
-    ts(("3", "vall", 144, 0, 24), ("3", "dli", 24, 0, 24), -1.0, None, A.mult)
-    ph[0] = 1.0
+    ts(("3", "vall", 0, 24), ("3", "dli", 0, 24), -1.0, None, A.mult)
     cp(("qa", 0, 72), ("qui", 0, 72))
     cp(("ntu", 0, 120), ("nti", 0, 120))
 
     def heads(s):
         o = (s + 1) * 48
         if s == S - 1:
-            cp(("cd", o, o + 24), ("qa", s * 24, s * 24 + 24))
+            scp(("cd", o, o + 24), ("qa", s * 24, s * 24 + 24))
             return
         tt(("cd", o, o + 24), ("nti", s * 24 + 24, s * 24 + 48), ("qa", s * 24, s * 24 + 24), A.subtract)
         tt(("cd", o + 24, o + 48), ("qa", s * 24 + 24, s * 24 + 48), ("qa", s * 24, s * 24 + 24), A.subtract)
 
+    TB, T0 = "py", 384
+
+    def sums(s0, s1):
+        lo, hi = (s0 + 1) * 24, (s1 + 1) * 24
+        o = (TB, T0, T0 + hi - lo)
+        a = max(s0, 0)
+        it = [(o, ID, ("k", "vall", k, lo, hi), k == 0, False) for k in range(8)]
+        it.append(((TB, T0 + (a - s0) * 24, T0 + hi - lo), ("i8", 0, 128), ("qa", a * 24, s1 * 24), False, True))
+        for z in range(0, 9, 3):
+            mm(it[z:z + 3], TB)
+        scp(("gs", lo, hi), o)
+
     def tails(s0, s1):
-        o = ("pb4", 384, 384 + 24 * (s1 - s0))
-        it = [(o, ID, ("qa", s0 * 24, s1 * 24), True, False)]
-        it += [(o, NID, ("k", "xall", 120, k, s0 * 24, s1 * 24), False, False) for k in range(8)]
-        it += [(o, ID, ("k", "vall", 144, k, s0 * 24 + 24, s1 * 24 + 24), False, k == 7) for k in range(8)]
-        for a, b in ((0, 5), (5, 9), (9, 13), (13, 17)):
-            mm(it[a:b])
-        act(("qa", s0 * 24 + 72, s1 * 24 + 72), o, F.Copy)
+        o = (TB, T0, T0 + 24 * (s1 - s0))
+        mm([(o, ID, ("qa", s0 * 24, s1 * 24), True, False), (o, NID, ("gs", s0 * 24, s1 * 24), False, False),
+            (o, ID, ("gs", s0 * 24 + 24, s1 * 24 + 24), False, True)], TB)
+        scp(("qa", s0 * 24 + 72, s1 * 24 + 72), o)
+
+    XP = 4 if C["x_by"] == "v" else 3
+
+    def lists(s, h):
+        c = (s + 1) * 24 + LC * h
+        return ("3", "vall", c, c + LC), ("pv", 2 * LW, 3 * LW), ("pv", (XP + h) * LW, (XP + h + 1) * LW)
 
     def post(s, h):
         n = "_%d" % h
-        v = ("3", "vall", 144, (s + 1) * 24 + 12 * h, (s + 1) * 24 + 12 * h + 12)
+        v, cb, xp = lists(s, h)
         o = (s + 1) * 48
-        cb, xp = ("pb6", 192, 288), ("pb6", 288 + 96 * h, 384 + 96 * h)
         if s == S - 1:
-            act(("bc" + n, 0, 96), ("i", ("cd", o, o + 24), ("ll" + n, 0, 6)), F.Copy)
-            act(cb, ("bc" + n, 0, 96), F.Copy)
-            tt(("3", "yds", 24, 12 * h, 12 * h + 12), cb, v, A.subtract)
+            scp(("bc" + n, 0, LW), ("i", ("cd", o, o + 24), ("ll", LC * h, LC * h + LC // 2)))
+            tt(("3", "yds", LC * h, LC * h + LC), ("bc" + n, 0, LW), v, A.subtract)
             return
-        act(("bc" + n, 0, 192), ("i", ("cd", o, o + 48), ("ll" + n, 0, 12)), F.Copy)
-        if PE_MOD and s >= 0:
-            mm([(cb, ID, ("bc" + n, 0, 96), True, False), (cb, ID, v, False, False)])
-            ops[-1]["wr"].append(("group6", 0, 1))
-            act(("su" + n, 0, 96), cb, F.Sign, bias=0.5)
-            mm([(cb, ("idk", 0, 128), ("su" + n, 0, 96), False, False), (cb, ("idb", 0, 128), ("kil", 0, 96), False, True)])
-            ops[-1]["wr"].append(("group6", 0, 1))
-            ops[-1]["cls"] = "t:mod"
-            cp(("off" + n, 0, 96), cb)
+        scp(("bc" + n, 0, 2 * LW), ("i", ("cd", o, o + 48), ("ll", LC * h, LC * h + LC)))
+        if s >= 0 and C["mod"]:
+            it = [(cb, ID, ("bc" + n, 0, LW), True, False), (cb, ID, v, False, True)]
+            mm(it, "pv")
+            ops[-1]["cls"] = "t:u"
+            act(("su" + n, 0, LW), cb, F.Sign, bias=0.5)
+            mm(it[:1] + [(cb, ID, v, False, False), (cb, ("idk", 0, 128), ("kil", 0, LW), False, False), (cb, ("idk", 0, 128), ("su" + n, 0, LW), False, True)], "pv")
+            ops[-1]["cls"] = "t:u"
+            cp(("off" + n, 0, LW), cb)
         else:
             if s < 0:
-                cp(("nh" + n, 0, 96), ("3", "dli", 24, 12 * h, 12 * h + 12))
-                tt(("ui" + n, 0, 96), ("i", ("cd", 0, 24), ("ll" + n, 0, 6)), ("nh" + n, 0, 96), A.subtract)
+                tag[1] = -1.0 + 0.4 * h
+                cp(("nh" + n, 0, LW), ("3", "dli", LC * h, LC * h + LC))
+                tt(("ui" + n, 0, LW), ("i", ("cd", 0, 24), ("ll", LC * h, LC * h + LC // 2)), ("nh" + n, 0, LW), A.subtract)
+            elif C["x_by"] == "t":
+                scp(cb, ("bc" + n, 0, LW))
+                tt(("ui" + n, 0, LW), cb, v, A.add)
             else:
-                act(cb, ("bc" + n, 0, 96), F.Copy)
-                tt(("ui" + n, 0, 96), cb, v, A.add)
-            ts(("uj" + n, 0, 96), ("ui" + n, 0, 96), 2047, None, A.bitwise_and)
-            cp(("off" + n, 0, 96), ("uj" + n, 0, 96))
-        if PE_X:
-            mm([(xp, ID, ("bc" + n, 96, 192), True, False), (xp, ID, v, False, True)])
-            ops[-1]["wr"].append(("group6", 0, 1))
-            ops[-1]["cls"] = "t:x"
+                scp(("pv", 2 * LW, 4 * LW), ("bc" + n, 0, 2 * LW))
+                tt(("ui" + n, 0, LW), cb, v, A.add)
+            ts(("uj" + n, 0, LW), ("ui" + n, 0, LW), 2047, None, A.bitwise_and)
+            cp(("off" + n, 0, LW), ("uj" + n, 0, LW))
+        if C["x_by"] == "t":
+            mm([(xp, ID, ("bc" + n, LW, 2 * LW), True, False), (xp, ID, v, False, True)], "pv")
+        elif s < 0:
+            tt(xp, ("bc" + n, LW, 2 * LW), v, A.add)
         else:
-            act(xp, ("bc" + n, 96, 192), F.Copy)
-            tt(xp, xp, v, A.add)
-        act(("aa" + n, 0, 96), xp, F.Abs)
-        act(("3", "xall", 120, (s + 1) * 24 + 12 * h, (s + 1) * 24 + 12 * h + 12), xp, F.Copy)
-        act(("ab" + n, 0, 96), ("aa" + n, 0, 96), F.Abs, bias=-1024.0)
-        act(("sg" + n, 0, 96), ("ab" + n, 0, 96), F.Sign, bias=-511.5)
+            tt(xp, ("pv", 3 * LW, 4 * LW), v, A.add)
+        act(("aa" + n, 0, LW), xp, F.Abs)
+        act(("ab" + n, 0, LW), ("i", ("aa" + n, 0, LW), ("turn", 0, LC // 2)), F.Abs, bias=-1024.0)
+        act(("sg" + n, 0, LW), ("ab" + n, 0, LW), F.Sign, bias=-511.5)
 
-    ring = [0, 0]
+    def bank(kind, s, h, lo, hi):
+        c = lo // BW
+        return ("%s_%d" % (kind, (NBK * (H * s + h) + c) % 2), lo - BW * c, hi - BW * c)
+
+    def late(s, h, lo):
+        return s == 0 and lo < C["direct"][h]
+
+    def wb_pieces(h, lo, hi):
+        cut = sorted(set([lo, hi] + [z for z in range(0, WP, NB) if lo < z < hi]))
+        return [(a, b, ("wb", (a // NB) * 384 + NB * h + a % NB, (a // NB) * 384 + NB * h + a % NB + b - a)) for a, b in pairs(cut)]
+
+    def wb_load(kind, h, lo, hi, stop):
+        mm([(bank(kind, 0, h, a, b), IDB, z, a == lo, stop and b == hi) for a, b, z in wb_pieces(h, lo, hi)], bank(kind, 0, h, lo, hi)[0])
+
+    def acc(s, h):
+        z = "pl_%d" % ((H * s + h) % 2 if H > 2 else 0)
+        return ("k", z, 0, 0, 2 * NB), ("k", z, 1, 0, 2 * NB)
+
+    def places(s, h):
+        if H > 2:
+            z = (H * s + h) % 2
+            e = {"pl": acc(s, h)[0], "py": ("py", 2 * NB, 3 * NB), "pv": ("pv", 384, 512)}[C["e_at"]]
+            return ("py", NB * z, NB * z + NB), e, acc(s, h)[1]
+        y = ("k", "pl_0", 0, 0, NB) if (s, h) == (0, 1) else ("py", 0, NB)
+        return y, ("py", BW - 2 * NB, BW), bank("st", s, h, BW, BW + 2 * NB)
+
+    def blocks(h):
+        return C["send"][h], C["send"][h + 1]
 
     def front(s, h):
         n = "_%d" % h
-        y = ("pb7", 0, NB)
-        ph[0] = 6 * s + 3 * h
-        win = ("rb", 0, 2048) if s == 0 else ("rr", 0, 2048)
-        for i in range(4):
-            lo = 384 * i
-            xr = "pb%d" % (ring[0] % 2)
-            ring[0] += 1
-            if s == 0 and i in V_GATH[h]:
-                cp(("x" + n, lo, lo + 384), ("i", win, ("off" + n, 24 * i, 24 * i + 24)))
-            else:
-                act(("x" + n, lo, lo + 384), ("i", win, ("off" + n, 24 * i, 24 * i + 24)), F.Copy)
-            act((xr, 0, 384), ("x" + n, lo, lo + 384), F.Copy)
-            if s == 0:
-                for u in range(2):
-                    c0 = (2 * i + u) * 384 + NB * h
-                    tt(("p" + n, lo + NB * u, lo + NB * u + NB), (xr, NB * u, NB * u + NB), ("wb", c0, c0 + NB), A.mult)
-            elif i == 3:
-                for u in range(2):
-                    tt(("p" + n, lo + NB * u, lo + NB * u + NB), (xr, NB * u, NB * u + NB), ("w" + n, lo + NB * u, lo + NB * u + NB), A.mult)
-            else:
-                tt(("p" + n, lo, lo + 384), (xr, 0, 384), ("w" + n, lo, lo + 384), A.mult)
-            it = [(y, NID, ("p" + n, lo, lo + NB), i == 0, False), (y, NID, ("p" + n, lo + NB, lo + 384), False, False)]
-            if i == 3:
-                c0 = s * 384 + NB * h
-                mm(it[:1])
-                it = [it[1], (y, ("idb", 0, 128), ("db", c0, c0 + NB), False, True)]
-            mm(it)
-        es, ep = ("es" + n, 0, NB), ("pb4", NB * h, NB * h + NB)
-        if E_PSUM:
-            ts(ep, y, -2.0, 2.0, A.max, A.min)
-            ops[-1]["cls"] = "v:es"
-            act(es, ep, F.Copy)
-        else:
-            ts(es, y, -2.0, 2.0, A.max, A.min)
-            act(ep, es, F.Copy)
+        phase("front", s, h)
+        y, e, _ = places(s, h)
         r = 16 * (1 + s)
         c0 = s * 384 + NB * h
-        for u in range(2):
-            mm([(("pb%d" % u, 384, 480), ("idf", 128 - r, 256 - r), ("es" + n, 96 * u, 96 * u + 96), True, True)])
-            act(("snd", c0 + 96 * u, c0 + 96 * u + 96), ("pb%d" % u, 384, 480), F.Copy)
+        win = ("rb", 0, 2048) if s == 0 else ("rr", 0, 2048)
+        for i, (lo, hi) in enumerate(pairs(C["gb"])):
+            (cp if s == 0 and i in C["v_gath"][h] else scp)(("x" + n, lo, hi), ("i", win, ("off" + n, lo // 16, hi // 16)))
+        k = 0
+        for lo, hi in pairs(C["pb"]):
+            if late(s, h, lo):
+                for a, b, z in wb_pieces(h, lo, hi):
+                    tt(("p" + n, a, b), ("x" + n, a, b), z, A.mult)
+            else:
+                if lo % BW == 0 and s > 0:
+                    scp(bank("st", s, h, lo, lo + BW), ("w" + n, lo, lo + BW))
+                elif lo % BW == 0:
+                    wb_load("st", h, lo, lo + BW, True)
+                tt(("p" + n, lo, hi), bank("st", s, h, lo, hi), ("x" + n, lo, hi), A.mult)
+            it = []
+            while NB * k + NB <= hi:
+                it.append((y, ("nidf", 128 - r, 256 - r), ("p" + n, NB * k, NB * k + NB), k == 0, False))
+                k += 1
+            if k == 8:
+                it.append((y, ("idb", 128 - r, 256 - r), ("db", c0, c0 + NB), False, True))
+            if it:
+                mm(it, regs(y)[0][0])
+                ops[-1]["cls"] = "t:py"
+        ts(("snd", c0, c0 + NB), y, -2.0, 2.0, A.max, A.min)
+        lo, hi = blocks(h)
+        if lo == hi:
+            return
 
         def send(q, T, X):
             core, rank, topo = X
             tr = []
-            for u in range(2):
-                b = 2 * h + u
+            for b in range(lo, hi):
                 dst = T.cores[(rank + 1 + b) % len(T.cores)]
                 rid, pid, _ = topo.addr(dst)
                 eng = topo.engines(core, dst)
-                half = len(eng) // 2
-                mask = sum(1 << e for e in eng[u * half:(u + 1) * half])
+                share = len(eng) // (hi - lo)
                 c = s * 384 + 96 * b
-                tr.append(RemoteDMATransfer(dst_ids=[DstId(rid=rid, pnc=pid)], dma_engine_mask=mask,
+                tr.append(RemoteDMATransfer(dst_ids=[DstId(rid=rid, pnc=pid)], dma_engine_mask=sum(1 << j for j in eng[share * (b - lo):share * (b - lo + 1)]),
                                             remote_sem=T.sem["arr%d_%d" % (s, h)], src=T.snd[:, c:c + 96], dst=T.land[:, c:c + 96]))
             return q.remote_dma_fused(tr, local_sem=T.sem.sent)
-        k = add("g", send, [], [("snd", c0, c0 + NB)], 300, "send")
-        add(None, None, [("land", c0, c0 + NB)], [], 3500, "recv", "arr%d_%d" % (s, h), after=k)
+        k = add("g", send, [], [("snd", s * 384 + 96 * lo, s * 384 + 96 * hi)], 360, "send")
+        add(None, None, [("land", s * 384 + 96 * lo, s * 384 + 96 * hi)], [], 0, "recv", "arr%d_%d" % (s, h), after=k)
 
-    def rest(s, h):
+    ring = [1]
+
+    def update(s, h):
         n = "_%d" % h
-        y = ("pb4", NB * h, NB * h + NB)
-        m0 = ("pb7", NB, 2 * NB)
-        ph[0] = 6 * s + 2 + 3 * h
-        far = DMA_UPD if s else ()
-        for i in far:
-            lo = 384 * i
-            tch, wch = ("t" + n, lo, lo + 384), ("w" + n, lo, lo + 384)
-            for u in range(2):
-                tt(("t" + n, lo + NB * u, lo + NB * u + NB), y, ("x" + n, lo + NB * u, lo + NB * u + NB), A.mult)
-            act(tch, tch, F.Copy, scale=0.015625)
-            add("g", lambda q, T, X, a=wch, b=tch: q.dma_start(ap(T, a), ap(T, b), accum_op=A.add), [wch], [wch, tch], GDMA,
-                "dma", "upd%d_%d_%d" % (s, h, i), 2 * 128 * 384 * 4)
-            act(("m" + n, lo, lo + 384), wch, F.Abs)
-            ops[-1]["cls"] = "s:far"
-        for i in range(4):
-            if i in far:
-                continue
-            lo = 384 * i
-            ur = "pb%d" % (2 + ring[1] % 2)
-            ring[1] += 1
-            for u in range(2):
-                tt(("t" + n, lo + NB * u, lo + NB * u + NB), y, ("x" + n, lo + NB * u, lo + NB * u + NB), A.mult)
-            tch, wch, mch = ("t" + n, lo, lo + 384), ("w" + n, lo, lo + 384), ("m" + n, lo, lo + 384)
-            wbs = [("wb", (2 * i + u) * 384 + NB * h, (2 * i + u) * 384 + NB * h + NB) for u in range(2)]
-            if i in PE_UPD:
+        phase("update", s, h)
+        _, e, m0 = places(s, h)
+        r, c0 = 16 * (1 + s), s * 384 + NB * h
+        reps = C["erep"] if C["e_by"] == "t" else 1
+        mm([(part(e, NB * z, NB * z + NB), ("idf", r, 128 + r), ("snd", c0, c0 + NB), z == 0, z == reps - 1) for z in range(reps)], regs(e)[0][0])
+        ops[-1]["cls"] = "t:e"
+        if reps < C["erep"]:
+            scp(part(e, NB, 2 * NB), part(e, 0, NB))
+            ops[-1]["cls"] = "s:e"
+        wd = NB * C["erep"]
+        for c in range(0, WP, wd):
+            tt(("t" + n, c, c + wd), part(e, 0, wd), ("x" + n, c, c + wd), A.mult)
+        cuts = [(BW * c, BW * c + BW, "T") for c in range(NBK)] if s == 0 else [z + (m,) for z, m in zip(pairs(C["ub"]), C["um"])]
+        wd = NB * C["lanes"]
+        taps = [(k + C["first"]) % 8 for k in range(8)]
+        for lo, hi, mode in cuts:
+            up, wv, tv = bank("up", s, h, lo, hi), ("w" + n, lo, hi), ("t" + n, lo, hi)
+            if C["fix"] and s > 0:
+                up = ("up_%d" % (ring[0] % 2), 0, hi - lo) if mode == "T" else bank("st", s, h, 0, hi - lo)
+                ring[0] += mode == "T"
+            if mode == "T":
                 if s == 0:
-                    mm([((ur, NB * u, NB * u + NB), ("idb", 0, 128), wbs[u], u == 0, False) for u in range(2)])
+                    wb_load("up", h, lo, hi, False)
                 else:
-                    mm([((ur, 0, 384), ID, wch, True, False)])
+                    mm([(up, ID, wv, True, False)], up[0])
                 ops[-1]["cls"] = "t:load"
-                mm([((ur, 0, 384), ("i64", 0, 128), tch, False, True)])
-                if i == 0:
-                    act(m0, (ur, 0, NB), F.Abs)
-                act(mch, (ur, 0, 384), F.Abs)
-                act(wch, (ur, 0, 384), F.Copy)
+                mm([(up, ("i64", 0, 128), tv, False, True)], up[0])
+                new = up
+            elif mode == "D":
+                act(tv, tv, F.Copy, scale=0.015625)
+                ops[-1]["cls"] = "s:far"
+                add("g", lambda q, T, X, a=wv, b=tv: q.dma_start(ap(T, a), ap(T, b), accum_op=A.add), [wv], [wv, tv], 1200, "dma",
+                    "upd%d_%d" % (s, h), 2 * 128 * (hi - lo) * 4)
+                new = wv
             else:
-                act((ur, 0, 384), tch, F.Copy, scale=0.015625)
-                if s == 0:
-                    for u in range(2):
-                        tt(("w" + n, lo + NB * u, lo + NB * u + NB), (ur, NB * u, NB * u + NB), wbs[u], A.add)
-                else:
-                    tt(wch, (ur, 0, 384), wch, A.add)
-                if i == 0:
-                    act(m0, ("w" + n, 0, NB), F.Abs)
-                act(mch, wch, F.Abs)
-        acc = [("pb5", 0, NB), ("pb5", NB, 2 * NB)]
-        ph[0] = 6 * s + 2.2 + 3 * h
-        for k in range(1, 8):
-            for e in range(2):
-                tt(acc[e], m0 if k == 1 else acc[e], ("m" + n, NB * k, NB * k + NB), A.max if e else A.min)
-        ph[0] = 6 * s + 4 + 3 * h
-        for part in (1, 0):
-            for k in range(4 * part, 4 * part + 4):
-                for e in range(2):
-                    tt(("eq" + n, (2 * k + e) * NB, (2 * k + e + 1) * NB), acc[e], ("m" + n, NB * k, NB * k + NB), A.is_equal)
-            o = ("pb6", 96 * part, 96 * part + 96)
-            it = [(o, ID, ("ec", 96 * part, 96 * part + 96), True, False)]
-            it += [(("pb6", 24 * k + 12, 24 * k + 24), ("idn", 0, 128), ("sg" + n, 12 * k, 12 * k + 12), False, False)
-                   for k in range(4 * part, 4 * part + 4)]
-            mm(it)
+                act(up, tv, F.Copy, scale=0.015625)
+                ops[-1]["cls"] = "s:up"
+                tt(wv, up, wv, A.add)
+                new = wv
+            if lo <= NB * taps[0] < hi:
+                act(part(m0, 0, wd), part(new, NB * taps[0] - lo, NB * taps[0] - lo + wd), F.Abs)
+                ops[-1]["cls"] = "s:m0"
+            for a, b in pairs(sorted(set([lo, hi] + [z for z in C["ab"] if lo < z < hi]))):
+                act(("m" + n, a, b), part(new, a - lo, b - lo), F.Abs)
+                if mode == "D":
+                    ops[-1]["cls"] = "s:mfar"
+            if mode == "T":
+                scp(wv, up)
+        phase("minmax", s, h)
+        m = lambda k, z=1: ("m" + n, NB * k, NB * (k + z))
+        both = list(zip(acc(s, h), (A.min, A.max)))
+        if C["lanes"] == 1:
+            for k in taps[1:]:
+                for a, op in both:
+                    tt(part(a, 0, NB), part(m0 if k == taps[1] else a, 0, NB), m(k), op)
+        else:
+            for k in (taps[2], taps[4]):
+                for a, op in both:
+                    tt(a, m0 if k == taps[2] else a, m(k, 2), op)
+            for z, (a, op) in enumerate(both):
+                tt(part(a, 0, NB), part(a, 0, NB), m(taps[6]), op)
+                tt(("sb" + n, NB * z, NB * z + NB), part(a, NB, 2 * NB), m(taps[7]), op)
+                ops[-1]["cls"] = "v:pl"
+            for z, (a, op) in enumerate(both):
+                tt(part(a, 0, NB), part(a, 0, NB), ("sb" + n, NB * z, NB * z + NB), op)
+        if C["rep"] == 2:
+            z = acc(s, h)[0][1]
+            scp(("3", z, NB, 2 * NB), ("3", z, 0, NB))
+
+    def vote(s, h):
+        n = "_%d" % h
+        phase("masks", s, h)
+        wd = NB * C["rep"]
+        for e in range(2):
+            for k in range(8):
+                tt(("c", "eq" + n, NB * e, NB * e + NB, k), part(acc(s, h)[e], 0, NB), ("m" + n, NB * k, NB * k + NB), A.is_equal)
+        o = ("pv", 0, 2 * LW)
+        it = [(o, IDB, ("eca", 0, 2 * LW), True, False), (("pv", 0, LW), IDB, ("ecb", 0, LW), False, False),
+              (("pv", LW, 2 * LW), ("idn", 0, 128), ("sg" + n, 0, LW), False, False)]
+        if C["base"]:
+            mm(it, "pv")
             ops[-1]["cls"] = "t:base"
-            ops[-1]["wr"].append(("group6", 0, 1))
-            mm([(o, ("z2", 15 - j, 143 - j), ("eq" + n, 1536 * part + j, 1536 * part + 1536, 16), False, j == 15) for j in range(16)])
-            ops[-1]["wr"].append(("group6", 0, 1))
-            if part:
-                act(("ssb" + n, 0, 96), o, F.Copy)
-        ph[0] = 6 * s + 5.1 + 3 * h
-        tt(("ta" + n, 0, 96), ("pb6", 0, 96), ("ssb" + n, 0, 96), A.max)
-        tt(("tb" + n, 0, 48), ("ta" + n, 0, 48), ("ta" + n, 48, 96), A.max)
-        tt(("tc" + n, 0, 24), ("tb" + n, 0, 24), ("tb" + n, 24, 48), A.max)
-        ts(("td" + n, 0, 24), ("tc" + n, 0, 24), 2047, None, A.bitwise_and)
-        tt(("gg" + n, 0, 12), ("td" + n, 0, 12), ("td" + n, 12, 24), A.max)
-        renew(n)
-        tt(("nh" + n, 0, 96), ("i", ("gg" + n, 0, 12), ("ll_0", 0, 6)), ("offc", 0, 96), A.not_equal)
-        tt(("3", "vall", 144, (s + 1) * 24 + 12 * h, (s + 1) * 24 + 12 * h + 12), ("pb6", 288 + 96 * h, 384 + 96 * h), ("nh" + n, 0, 96), A.mult)
+            it = []
+        mm(it + [(o, ("z2", 15 - j, 143 - j), ("j", "eq" + n, j), False, j == 15) for j in range(16)], "pv")
+        phase("lists", s, h)
+        vec(lambda q, T, X: q.tensor_tensor_scan(T["ta" + n][:, :], T.keep[:, :], ap(T, o), 0.0, A.mult, A.max),
+            ("ta" + n, 0, 2 * LW), [o, ("keep", 0, 2 * LW)])
+        tt(("tc" + n, 0, LC), ("ta" + n, 7, LW, 8), ("ta" + n, LW + 7, 2 * LW, 8), A.add)
+        ts(("gg" + n, 0, LC), ("tc" + n, 0, LC), TIE - 1, None, A.bitwise_and)
+        cp(("wo" + n, 0, LC), ("gg" + n, 0, LC))
+        act(("i", ("w" + n, 0, 2 * WP), ("wo" + n, 0, LC)), ("quart", 0, NB), F.Sigmoid)
+        tt(("nh" + n, 0, LW), ("i", ("gg" + n, 0, LC), ("ll", 0, LC // 2)), ("offc", 0, LW), A.not_equal)
+        v, _, xp = lists(s, h)
+        tt(v, xp, ("nh" + n, 0, LW), A.mult)
         post(s, h)
 
+    def scatter(s):
+        for h in range(H):
+            phase("scatter", s, h)
+            lo, hi = blocks(h)
+            if lo < hi:
+                cp(("i", ("rr", 0, 2048), ("ntu", s * 24 + 6 * lo, s * 24 + 6 * hi)), ("land", s * 384 + 96 * lo, s * 384 + 96 * hi))
+
     for h in range(H):
-        ph[0] = h - 1.0
         post(-1, h)
-    ph[0] = 1.0
+    tag[1] = 0.1
     heads(0)
     heads(1)
     for s in range(S):
         for h in range(H):
-            front(s, h)
-        if s == 2:
-            tails(0, 2)
-            heads(2)
-            heads(3)
-            heads(4)
-        if s == 4:
-            tails(2, 4)
-        for h in range(H):
-            c0 = s * 384 + NB * h
-            ph[0] = 6 * s + (5.3 if h else 4.5)
-            if s < S - 1:
-                cp(("i", ("rr", 0, 2048), ("ntu", s * 24 + 12 * h, s * 24 + 12 * h + 12)), ("land", c0, c0 + NB))
-        for h in range(H):
-            rest(s, h)
-            if s == S - 1:
-                for k in range(8):
-                    store("y" if h == 0 or k % 2 else "s", "yw", k * 384 + NB * h, k * 384 + NB * h + NB, ("w_%d" % h, NB * k, NB * k + NB))
+            if (s, h) == (0, 0):
+                front(0, 0)
+                front(0, 1)
+            update(s, h)
+            if h == H - 1 and s < S - 1:
+                scatter(s)
+                front(s + 1, 0)
+            elif h < H - 1 and (s, h) != (0, 0):
+                front(s, h + 1)
+            if h == 0 and s in (2, 4):
+                phase("tails", s, h)
+                sums(-1 if s == 2 else 2, s)
+                tails(s - 2, s)
+                if s == 2:
+                    for z in (2, 3, 4):
+                        heads(z)
+            vote(s, h)
+    tag[:] = ["end", 1000.0]
+    for h in range(H):
+        for k in range(8):
+            store("y" if h < H - 1 or k % 2 else "s", "yw", k * 384 + NB * h, k * 384 + NB * h + NB, ("w_%d" % h, NB * k, NB * k + NB))
     store("y", "yr", 0, 384, ("land", 1536, 1920))
-    tails(4, 5)
-    store("y", "yd", 0, 192, ("3", "yds", 24, 0, 24))
+    o = ("up_0", 0, 24)
+    mm([(o, ID, ("qa", 96, 120), True, False), (o, ("i8", 0, 128), ("qa", 96, 120), False, False), (o, NID, ("gs", 96, 120), False, False)], "up_0")
+    mm([(o, ID, ("k", "vall", k, 120, 144), False, k == 7) for k in range(8)], "up_0")
+    scp(("qa", 168, 192), o)
+    store("y", "yd", 0, 192, ("3", "yds", 0, 24))
     store("s", "yq", 0, 72, ("qa", 120, 192))
     return ops
 
@@ -503,57 +645,82 @@ def edges(ops):
 
 def schedule(ops, data):
     n = len(ops)
+    C = CFG
+    lam = C["lam"]
     pred, succ = [set(p) for p in data[0]], data[1]
-    dur = [o["cost"] + (2000 + o["bytes"] / 180.0 if o["kind"] == "dma" else 0) for o in ops]
-    due, t = [0.0] * n, 0.0
-    for i in sorted(range(n), key=lambda z: (ops[z]["ph"], z)):
-        due[i] = t if ops[i]["eng"] == "v" else 1e9
-        t += ops[i]["cost"] if ops[i]["eng"] == "v" else 0.0
-    for i in range(n - 1, -1, -1):
-        due[i] = min([due[i], t + 1e4 - dur[i]] + [due[j] - dur[i] - LAM for j in succ[i]])
-    prio = [LEAD.get(ops[i]["cls"], 0.0) - due[i] for i in range(n)]
+    cost = [o["cost"] * C["cy"] + (C["ovh"] if o["eng"] in ("v", "s") else C["tovh"] * o["nins"] if o["eng"] == "t" else 0.0) for o in ops]
+    prio, seen = [], {}
+    for i, o in enumerate(ops):
+        z = o["tag"].split()
+        if len(z) == 1:
+            prio.append(-(10 * o["ph"] + 1e-4 * i))
+            continue
+        k = seen[o["tag"], o["cls"]] = seen.get((o["tag"], o["cls"]), -1) + 1
+        at = C["round"].get(z[0] + " " + o["cls"], C["round"][z[0]])
+        at += C["pace"].get(z[0] + " " + o["cls"], C["pace"].get(z[0], 0.0)) * k + C["shift"][z[0]][int(z[2])]
+        if z[1] in "04":
+            at += C["shift"].get(z[0] + z[1], [0.0] * H)[int(z[2])]
+        prio.append(-(C["step"] * int(z[1]) + at + 1e-4 * i))
+    line = {e: sorted((i for i in range(n) if ops[i]["eng"] == e and ops[i]["tag"] != "start"), key=lambda z: prio[z]) for e in C["win"]}
+    done = set()
     left = [len(p) for p in pred]
-    ready = [i for i in range(n) if left[i] == 0]
-    free = {"v": 0.0, "s": 0.0, "t": 0.0, "g": 0.0, "y": 0.0, None: 0.0}
+    ready = {e: [i for i in range(n) if left[i] == 0 and ops[i]["eng"] == e] for e in ("v", "s", "t", "g", "y", None)}
+    free = {e: 0.0 for e in ready}
     fin, start, base = [0.0] * n, [0.0] * n, [0.0] * n
-    bank, order, wire = {}, [], 0.0
-    while ready:
-        can = []
-        for i in ready:
-            o = ops[i]
-            t = max(free[o["eng"]], base[i])
-            for b in o["banks"]:
-                for e, j in bank.get(b, {}).items():
-                    if e != o["eng"]:
-                        t = max(t, fin[j] + LAM)
-            can.append((t, i))
-        t0, i0 = min(can)
-        e0 = ops[i0]["eng"]
-        _, i, t = min((-prio[i], i, t) for t, i in can if ops[i]["eng"] == e0 and t <= t0 + LOOK.get(e0, 0.0))
+    bank, order, wire, busy = {}, [], 0.0, set()
+
+    def when(i):
+        e0 = ops[i]["eng"]
+        t = max(free[e0], base[i])
+        for b in ops[i]["banks"]:
+            for e, j in bank.get(b, {}).items():
+                if e != e0 and fin[j] + lam > t:
+                    t = fin[j] + lam
+        return t
+    for _ in range(n):
+        best = None
+        for e, lst in ready.items():
+            if e == "t":
+                lst = [i for i in lst if not (ops[i]["group"][1] and ops[i]["group"][0] in busy)]
+            if line.get(e):
+                least = prio[line[e][-1]] - C["win"][e]
+                lst = [i for i in lst if prio[i] >= least or ops[i]["tag"] == "start"]
+            if lst:
+                can = [(when(i), i) for i in lst]
+                if best is None or min(can)[0] < best[0]:
+                    best = (min(can)[0], e, can)
+        if best is None:
+            i = max((i for e, lst in ready.items() for i in lst if e != "t"), key=lambda z: prio[z])
+            best = (when(i), ops[i]["eng"], [(when(i), i)])
+        t0, e0, can = best
+        _, i, t = min((-prio[i], i, t) for t, i in can if t <= t0 + C["look"].get(e0, 0.0))
         o = ops[i]
-        ready.remove(i)
+        ready[e0].remove(i)
+        if e0 == "t":
+            (busy.discard if o["group"][2] else busy.add)(o["group"][0])
+        done.add(i)
+        while line.get(e0) and line[e0][-1] in done:
+            line[e0].pop()
         for b in o["banks"]:
             for e, j in bank.setdefault(b, {}).items():
                 if e != o["eng"]:
                     pred[i].add(j)
             bank[b][o["eng"]] = i
         start[i] = t
-        fin[i] = t + o["cost"]
+        fin[i] = t + cost[i]
         if o["eng"] is not None:
             free[o["eng"]] = fin[i]
         if o["kind"] == "dma":
-            if o["bytes"] > 98000 and o["sem"] != "l_dl":
-                wire = max(wire, fin[i]) + o["bytes"] / 180.0
-                fin[i] = wire + 2000
-            else:
-                fin[i] += 2000 + o["bytes"] / 180.0
+            wire = max(wire, fin[i] + 1500) + o["bytes"] / 180.0
+            fin[i] = wire + 500
+        if o["kind"] == "recv":
+            fin[i] += C["rem"]
         order.append(i)
         for j in succ[i]:
-            both_pe = o["eng"] == "t" and ops[j]["eng"] == "t"
-            base[j] = max(base[j], fin[i] + (0.0 if both_pe else LAM))
+            base[j] = max(base[j], fin[i] + (0.0 if e0 == "t" and ops[j]["eng"] == "t" else lam))
             left[j] -= 1
             if left[j] == 0:
-                ready.append(j)
+                ready[ops[j]["eng"]].append(j)
     return order, pred, start, fin
 
 
@@ -577,10 +744,9 @@ def waits(ops, order, pred):
                 continue
             lst.append(j)
             kn[key] = val
-            if TRANS:
-                for k2, v2 in clock[j].items():
-                    if kn.get(k2, 0) < v2:
-                        kn[k2] = v2
+            for k2, v2 in clock[j].items():
+                if kn.get(k2, 0) < v2:
+                    kn[k2] = v2
         need[i] = lst
         raised.update(lst)
         clock[i] = dict(kn)
@@ -595,7 +761,9 @@ def waits(ops, order, pred):
         if o["kind"] == "c" and i in raised:
             count[o["eng"]] = count.get(o["eng"], 0) + 1
             val[i] = (ESEM[o["eng"]], count[o["eng"]])
-        elif o["kind"] in ("dma", "recv"):
+        elif o["kind"] == "dma":
+            val[i] = (o["sem"], 16 * sum(z["sem"] == o["sem"] for z in ops))
+        elif o["kind"] == "recv":
             val[i] = (o["sem"], 16)
     return need, val
 
@@ -620,21 +788,19 @@ def rank_program(g, core, T, topo):
     ops, need, val = P["ops"], P["need"], P["val"]
     Q = {"v": g.vector, "s": g.scalar, "t": g.tensor, "g": g, "y": g.sync}
     X = (core, rank, topo)
-    stores = sends = 0
+    stores = 0
     for i in P["order"]:
         o = ops[i]
         if o["kind"] == "recv":
             continue
         q = Q[o["eng"]]
-        for j in need[i]:
-            q.wait_ge(T.sem[val[j][0]], val[j][1])
+        for name, count in sorted(set(val[j] for j in need[i])):
+            q.wait_ge(T.sem[name], count)
         ins = o["fn"](q, T, X)
         if o["kind"] == "dma":
             ins.then_inc(T.sem[o["sem"]], 16)
             stores += o["sem"] == "out"
-        elif o["kind"] == "send":
-            sends += 1
-        elif i in val:
+        elif i in val and o["kind"] == "c":
             ins.then_inc(T.sem[val[i][0]], 1)
-    g.wait_ge(T.sem.sent, 16 * sends)
+    g.wait_ge(T.sem.sent, 16 * sum(o["kind"] == "send" for o in ops))
     g.wait_ge(T.sem.out, 16 * int(stores))

from concourse.bass import DstId, RemoteDMATransfer
from concourse.mybir import AluOpType as A, ActivationFunctionType as F, AxisListType

S, H = 5, 3
NB = 384 // H
LC = NB // 16
WP, LW = 8 * NB, 8 * LC
TIE = 2048 if 9 * NB > 1024 else 1024
BW = 512
NBK = WP // BW
CFG = {
    "gb": tuple(range(0, WP + 1, 512)),
    "pb": tuple(range(0, WP + 1, 512)),
    "ub": (0, 512, 1024, 1152, 1536) if H == 2 else (0, 512, 768, 1024), "um": "TTTV" if H == 2 else "TTV",
    "ab": tuple(range(0, WP + 1, 512)),
    "vg": (0, 2, 4),
    "erep": 2, "e_by": "t", "lanes": 2, "rep": 2, "e_at": "py", "mod": False, "base": False, "x_by": "t", "first": 0, "fix": True,
    "v_gath": ((1,), (1,), (), ()),
    "send": (0, 2, 4) if H == 2 else (0, 0, 2, 4), "direct": (0, 0, 0, 0), "rr": 1.0,
    "cy": 0.83, "lam": 200.0, "ovh": 20.0, "tovh": 0.0, "wl": False, "gath": 1.55, "scat": 3.8, "rem": 5000.0,
    "look": {"v": 0.0, "s": 0.0, "t": 0.0},
    "win": {"v": 2.0}, "step": 18.0,
    "shift": {"front": [0.0, 9.0], "update": [4.0, 13.0], "minmax": [6.0, 15.0], "masks": [8.2, 17.2],
              "lists": [13.5, 22.5], "scatter": [13.0, 17.0], "tails": [8.0, 0], "front0": [0, -4.0]} if H == 2 else
             {"front": [-0.5, 3.8, 8.0], "update": [3.0, 8.3, 14.1], "minmax": [6.5, 11.6, 17.6], "masks": [7.9, 14.1, 20.1],
              "lists": [12.3, 17.2, 22.9], "scatter": [15.2, 12.4, 18.3], "tails": [10.9, 5.2, 2.4], "front0": [-0.7, -3.3, -3.9]},
    "round": {
        "front": 0.0, "front s:st": -1.5, "front s:x": -2.0, "front v:snd": 2.6, "front t:py": 0.3,
        "update": 0.0, "update s:m0": 1.0, "update s:m": 1.1, "update s:w": 5.0, "update t:up": 0.5, "update t:load": -1.0,
        "update t:e": -1.0, "update s:e": -1.0, "update s:up": 1.0, "update v:w": 1.3,
        "minmax": 0.0, "minmax s:pl": 0.0, "masks": 0.0, "masks t:pv": 1.5, "masks s:ssb": 2.0,
        "lists": 0.0, "lists s:w": 1.5, "lists s:bc": -2.0, "lists s:pv": -1.0, "lists t:pv": 2.5,
        "lists s:aa": 4.0, "lists s:ab": 4.2, "lists s:sg": 4.4, "lists v:tb": 0.25, "lists v:tc": 0.5, "lists v:td": 0.75,
        "lists v:gg": 1.0, "lists v:wo": 1.25, "lists v:nh": 1.3, "lists v:vall": 1.65, "lists v:ui": 1.9, "lists v:uj": 2.15,
        "lists v:off": 2.4, "lists v:yds": 1.9, "scatter": 0.0, "tails": 0.0,
    },
    "pace": {"front v:p": 0.8, "front s:x": 0.8, "front s:st": 0.8, "front t:py": 0.8, "update v:t": 0.1, "minmax": 0.25, "masks v:eq": 0.5,
             "masks t:pv": 1.4, "update s:m": 0.8, "update t:up": 0.8, "update s:w": 0.4},
}

CFG.update({'round': {'front': 0.1, 'front s:st': 1.6, 'front s:x': 1.6, 'front v:snd': 2.3, 'front t:py': 0.9, 'update': 0.6, 'update s:m0': 2.4, 'update s:m': 1.0, 'update s:w': 6.1, 'update t:up': 0.2, 'update t:load': 0.5, 'update t:e': -1.7, 'update s:e': -2.2, 'update s:up': 4.1, 'update v:w': 2.5, 'minmax': 0.0, 'minmax s:pl': -0.8, 'masks': 1.3, 'masks t:pv': 4.5, 'masks s:ssb': -7.2, 'lists': -0.4, 'lists s:w': 2.9, 'lists s:bc': -8.9, 'lists s:pv': 4.3, 'lists t:pv': 1.5, 'lists s:aa': -1.4, 'lists s:ab': 4.1, 'lists s:sg': 8.5, 'lists v:tb': -0.25, 'lists v:tc': 1.5, 'lists v:td': 1.25, 'lists v:gg': -0.3, 'lists v:wo': 1.45, 'lists v:nh': 1.6, 'lists v:vall': 2.25, 'lists v:ui': 2.2, 'lists v:uj': 3.35, 'lists v:off': 2.3, 'lists v:yds': 1.9, 'scatter': -2.7, 'tails': 0.2}, 'pace': {'front v:p': 2.25, 'front s:x': 2.025, 'front s:st': 0.95, 'front t:py': 1.19, 'update v:t': 0.045, 'minmax': 0.245, 'masks v:eq': 0.22, 'masks t:pv': 0.275, 'update s:m': 2.315, 'update t:up': 1.05, 'update s:w': 1.135}, 'shift': {'front': [-0.2, 3.9, 8.4], 'update': [1.9, 7.9, 13.7], 'minmax': [6.9, 11.1, 18.6], 'masks': [8.4, 14.1, 19.9], 'lists': [12.8, 18.5, 22.0], 'scatter': [14.0, 17.4, 21.9], 'tails': [8.9, 7.2, 2.1], 'front0': [-2.5, -2.4, -3.4], 'update0': [2.4, 0.0, 0.6], 'minmax0': [-0.9, 0.8, 0.1], 'masks0': [-0.3, 0.5, 0.7], 'front4': [1.7, 0.2, -3.3], 'update4': [-0.2, -0.8, 1.8], 'minmax4': [-1.5, 0.5, 1.0], 'masks4': [-0.9, 2.0, 1.6], 'lists4': [4.3, 0.9, 1.4]}, 'ub': (0, 512, 1024), 'um': 'TV', 'e_by': 't', 'ovh': 0, 'm0': False, 'lam': 200, 'rem': 4000, 'vg': (0, 2, 4), 'win': {'v': 3, 's': 100}, 'look': {'v': 0, 's': 0, 't': 150}, 'fix': False, 'direct': (0, 0, 0, 0), 'gb': (0, 512, 1024), 'pb': (0, 512, 1024), 'v_gath': ((1,), (), (), ()), 'step': 18})

CFG.update({'round': {'front': 0.1, 'front s:st': -0.4, 'front s:x': 3.4, 'front v:snd': 1.7, 'front t:py': 1.8, 'update': -0.4, 'update s:m0': 2.0, 'update s:m': 4.6, 'update s:w': 8.0, 'update t:up': 0.2, 'update t:load': -0.4, 'update t:e': -1.4, 'update s:up': 5.0, 'update v:w': 2.1, 'minmax': 0.0, 'masks': 1.3, 'masks t:pv': 6.4, 'lists': 1.3, 'lists s:w': 5.1, 'lists s:bc': -8.5, 'lists s:pv': 3.9, 'lists t:pv': 2.8, 'lists s:aa': -0.9, 'lists s:ab': 5.7, 'lists s:sg': 9.5, 'lists v:tc': 1.4, 'lists v:gg': -0.6, 'lists v:wo': 2.25, 'lists v:nh': 2.3, 'lists v:vall': 2.05, 'lists v:ui': 0.4, 'lists v:uj': 1.95, 'lists v:off': 1.9, 'lists v:yds': 1.1, 'scatter': -1.4, 'tails': 1.2, 'masks t:base': 1.5, 'lists v:pv': 5.7}, 'rep': 1, 'erep': 1, 'pace': {'front v:p': 2.325, 'front s:x': 2.175, 'front s:st': 0.26, 'front t:py': 0.785, 'update v:t': 0, 'minmax': 0.275, 'masks v:eq': 0.085, 'update s:m': 2.45, 'update t:up': 1.815, 'update s:w': 0.865}, 'shift': {'front': [0.4, 3.8, 8.0], 'update': [2.1, 7.6, 14.0], 'minmax': [7.1, 9.9, 17.8], 'masks': [8.4, 15.0, 19.6], 'lists': [13.8, 18.6, 22.4], 'scatter': [16.3, 17.3, 22.6], 'tails': [10.2, 6.2, 2.8], 'front0': [-1.0, -1.3, -3.0], 'update0': [2.6, -0.2, 1.2], 'minmax0': [-0.5, 4.4, 0.4], 'masks0': [0.1, -0.5, 0.3], 'front4': [-1.0, -0.1, -3.2], 'update4': [1.3, -3.7, 0.8], 'minmax4': [-4.2, -2.4, -0.4], 'masks4': [-3.1, 0.7, 0.2], 'lists4': [2.3, 0.9, -0.5]}, 'base': True, 'x_by': 'v', 'e_at': 'pl', 'wl': True, 'win': {'v': 4, 's': 100}})

f32, bf16, i32, u16 = "float32", "bfloat16", "int32", "uint16"
SCRATCH = {
    "rb": ("sbuf", [128, 2048], bf16), "rr": ("sbuf", [128, 2048], f32), "wb": ("sbuf", [128, 3072], bf16),
    "db": ("sbuf", [128, 1920], bf16), "dli": ("sbuf", [128, 8, 24], i32), "nti": ("sbuf", [128, 120], i32),
    "qui": ("sbuf", [128, 72], i32), "ntu": ("sbuf", [128, 120], u16), "qa": ("sbuf", [128, 192], f32),
    "cd": ("sbuf", [128, 288], f32), "vall": ("sbuf", [128, 8, 144], f32), "gs": ("sbuf", [128, 144], f32),
    "yds": ("sbuf", [128, 8, 24], f32), "snd": ("sbuf", [128, 1920], f32), "land": ("sbuf", [128, 1920], f32),
    "ll": ("sbuf", [128, 24], u16), "e3": ("sbuf", [128, LW], f32), "idk": ("sbuf", [128, 128], bf16), "kil": ("sbuf", [128, LW], bf16),
    "keep": ("sbuf", [128, 2 * LW], f32), "jg": ("sbuf", [128, 4], f32), "turn": ("sbuf", [128, 8], u16),
    "ones": ("sbuf", [128, 256], f32), "idf": ("sbuf", [128, 256], f32), "nidf": ("sbuf", [128, 256], f32),
    "i64": ("sbuf", [128, 128], f32), "idb": ("sbuf", [128, 256], bf16), "idn": ("sbuf", [128, 128], bf16),
    "i8": ("sbuf", [128, 128], f32),
    "z2": ("sbuf", [128, 144], bf16), "t8a": ("sbuf", [128, 8], f32), "t8b": ("sbuf", [128, 8], f32),
    "t8c": ("sbuf", [128, 8], f32), "pj": ("sbuf", [128, 4], i32), "pk": ("sbuf", [128, 4], i32), "jf": ("sbuf", [128, 4], f32),
    "e1": ("sbuf", [128, LW], f32), "e2": ("sbuf", [128, 2 * LW], f32), "eca": ("sbuf", [128, 2 * LW], bf16),
    "ecb": ("sbuf", [128, 2 * LW], bf16), "offc": ("sbuf", [128, LW], f32), "lb": ("sbuf", [128, 24], f32),
    "lc": ("sbuf", [128, 24], i32), "ld": ("sbuf", [128, 24], f32), "le": ("sbuf", [128, 24], f32), "quart": ("sbuf", [128, 256], f32),
    "za": ("sbuf", [128, 128], f32), "zb": ("sbuf", [128, 128], f32),
}
for _h in range(H):
    for _n, _c, _d in (("w", [2 * WP], f32), ("x", [WP], f32), ("p", [WP], f32), ("t", [WP], f32), ("m", [WP], f32),
                       ("eq", [2 * NB, 8], bf16), ("sb", [2 * NB], f32), ("off", [LW], u16), ("ui", [LW], i32), ("uj", [LW], i32),
                       ("ssb", [LW], f32), ("ta", [2 * LW], f32), ("tb", [2, 2 * LC], f32), ("tc", [2 * LC], i32), ("td", [2 * LC], i32),
                       ("gg", [16], i32), ("wo", [LC], u16), ("nh", [LW], f32), ("bc", [2 * LW], f32), ("aa", [LW], f32),
                       ("ab", [LW], f32), ("sg", [LW], bf16), ("su", [LW], bf16)):
        SCRATCH[_n + "_%d" % _h] = ("sbuf", [128] + _c, _d)
for _b in ("st_0", "st_1", "up_0", "up_1", "py"):
    SCRATCH[_b] = ("psum", [128, BW], f32)
SCRATCH["pv"] = ("psum", [128, BW], f32)
for _b in range(1 if H == 2 else 2):
    SCRATCH["pl_%d" % _b] = ("psum", [128, 2, BW if H == 2 else BW // 2], f32)

LOADS = ["l_rb", "l_n0", "l_dl", "l_nt", "l_qu", "l_w0", "l_w1", "l_w2", "l_w3", "l_d0", "l_d1"]
SEMAPHORES = ["ev", "es", "et", "eg", "sent", "out"] + LOADS + ["upd%d_%d" % (s, h) for s in range(1, S) for h in range(H)] + ["arr%d_%d" % (s, h) for s in range(S) for h in range(H)]
ESEM = {"v": "ev", "s": "es", "t": "et", "g": "eg"}


def ap(T, a):
    if a[0] == "3":
        return T[a[1]][:, :, a[2]:a[3]]
    if a[0] == "k":
        return T[a[1]][:, a[2], a[3]:a[4]]
    if a[0] == "r":
        return T[a[1]][:, a[2]:a[3], :]
    if a[0] == "c":
        return T[a[1]][:, a[2]:a[3], a[4]]
    if a[0] == "j":
        return T[a[1]][:, a[2]::16, :]
    if a[0] == "i":
        return ap(T, a[1]).indirect(ap(T, a[2]))
    if len(a) == 4:
        return T[a[0]][:, a[1]:a[2]:a[3]]
    return T[a[0]][:, a[1]:a[2]]


def regs(a):
    if a[0] == "3":
        n, w = SCRATCH[a[1]][1][1:]
        return [(a[1], k * w + a[2], k * w + a[3]) for k in range(n)]
    if a[0] == "k":
        w = SCRATCH[a[1]][1][2]
        return [(a[1], a[2] * w + a[3], a[2] * w + a[4])]
    if a[0] == "r":
        w = SCRATCH[a[1]][1][2]
        return [(a[1], a[2] * w, a[3] * w)]
    if a[0] == "c":
        return [(a[1], a[4] * 2 * NB + a[2], a[4] * 2 * NB + a[3])]
    if a[0] == "j":
        return [(a[1], 0, 2 * WP)]
    if a[0] == "i":
        return regs(a[1])
    return [(a[0], a[1], a[2])]


def cnt(a):
    if a[0] == "i":
        return 16 * cnt(a[2])
    if a[0] == "j":
        return NB
    if len(a) == 4 and a[0] in SCRATCH:
        return len(range(a[1], a[2], a[3]))
    return sum(z[2] - z[1] for z in regs(a))


def psum(a):
    return SCRATCH[regs(a)[0][0]][0] == "psum"


def wide(a):
    return SCRATCH[regs(a)[0][0]][2] in (f32, i32)


def part(a, lo, hi):
    return a if a[0] == "r" else a[:-2] + (a[-2] + lo, a[-2] + hi)


def pairs(b):
    return list(zip(b[:-1], b[1:]))


def program():
    C = CFG
    ops = []
    tag = ["start", -1.0]

    def phase(name, s, h):
        tag[0] = "%s %d %d" % (name, s, h)

    def add(eng, fn, outs, ins, cost, kind="c", sem=None, nbytes=0, after=None, ind=None, group=None, nins=1):
        rd, wr = [], []
        for a in ins:
            rd += regs(a)
            if a[0] == "i":
                rd += regs(a[2])
        for a in outs:
            wr += regs(a)
            if a[0] == "i":
                rd += regs(a[2])
        banks = sorted(set((r[0], r[1] // BW) for r in rd + wr if SCRATCH[r[0]][0] == "psum"))
        ops.append({"group": group, "eng": eng, "fn": fn, "rd": rd, "wr": wr, "cost": cost, "kind": kind, "sem": sem, "bytes": nbytes,
                    "after": after, "banks": banks, "ind": ind, "tag": tag[0], "ph": tag[1], "nins": nins,
                    "cls": "%s:%s" % (eng, (wr + rd)[0][0].split("_")[0])})
        return len(ops) - 1

    def vec(fn, o, ins, two=False):
        if o[0] == "i":
            add("v", fn, [o], ins, 60 + C["scat"] * cnt(o), ind="s")
        elif ins and ins[0][0] == "i":
            add("v", fn, [o], ins, 60 + C["gath"] * cnt(o), ind="g")
        else:
            half = not two and not wide(o) and not any(wide(a) for a in ins[:1])
            add("v", fn, [o], ins, max(64, cnt(o) * (2 if two else 0.5 if half else 1)))
            ops[-1]["raw"] = cnt(o) * (2 if two else 0.5 if half else 1)

    def tt(o, a, b, op):
        vec(lambda q, T, X: q.tensor_tensor(ap(T, o), ap(T, a), ap(T, b), op), o, [a, b], not (psum(a) or psum(b)))

    def ts(o, a, s1, s2, op0, op1=None):
        def fn(q, T, X):
            z1 = ap(T, s1) if isinstance(s1, tuple) else s1
            if op1 is None:
                return q.tensor_scalar(ap(T, o), ap(T, a), z1, None, op0)
            return q.tensor_scalar(ap(T, o), ap(T, a), z1, s2, op0, op1)
        vec(fn, o, [a] + [z for z in (s1, s2) if isinstance(z, tuple)])

    def cp(o, a):
        vec(lambda q, T, X: q.tensor_copy(ap(T, o), ap(T, a)), o, [a])

    def ms(o, c):
        vec(lambda q, T, X: q.memset(ap(T, o), c), o, [])

    def act(o, a, func, bias=None, scale=None):
        def fn(q, T, X):
            if scale is not None:
                return q.activation(ap(T, o), ap(T, a), func, scale=ap(T, scale) if isinstance(scale, tuple) else scale)
            if bias is not None:
                return q.activation(ap(T, o), ap(T, a), func, bias=ap(T, bias) if isinstance(bias, tuple) else bias)
            return q.activation(ap(T, o), ap(T, a), func)
        if o[0] == "i":
            add("s", fn, [o], [a], 78 + C["scat"] * cnt(o), ind="s")
        elif a[0] == "i":
            add("s", fn, [o], [a], 78 + C["gath"] * cnt(o), ind="g")
        else:
            add("s", fn, [o], [a] + [z for z in (bias, scale) if isinstance(z, tuple)], max(64, cnt(o)))
            ops[-1]["raw"] = cnt(o)

    def scp(o, a):
        act(o, a, F.Copy)

    def mm(items, group=None):
        def fn(q, T, X):
            for o, l, r, st, sp in items:
                last = q.matmul(ap(T, o), ap(T, l), ap(T, r), st, sp)
            return last
        add("t", fn, [z[0] for z in items], [z[1] for z in items] + [z[2] for z in items] + [z[0] for z in items if not z[3]],
            sum(max(64, cnt(z[2])) * (2 if wide(z[2]) else 0.5) for z in items),
            group=(regs(items[0][0])[0][0], items[0][3], items[-1][4]), nins=len(items))
        ops[-1]["raw"] = sum(cnt(z[2]) * (2 if wide(z[2]) else 0.5) for z in items)

    def iota(o, pat, base, cm):
        def fn(q, T, X):
            if SCRATCH[o[0]][2] == i32:
                return q.iota(ap(T, o), pat, base, cm)
            return q.iota(ap(T, o), pat, base, cm, allow_small_or_imprecise_dtypes=True)
        add("g", fn, [o], [], 160 + 2 * cnt(o))

    def sel(o, a, pat, op, base, cm):
        add("g", lambda q, T, X: q.affine_select(ap(T, o), ap(T, a), pat, op, 0.0, base, cm), [o], [a], 200 + 2 * cnt(o))

    def load(eng, o, name, lo, hi, sem, size):
        add(eng, lambda q, T, X: q.dma_start(ap(T, o), T[name][:, lo:hi]), [o], [], 70, "dma", sem, 128 * (hi - lo) * size)

    def store(eng, name, lo, hi, a):
        add(eng, lambda q, T, X: q.dma_start(T[name][:, lo:hi], ap(T, a)), [], [a], 70, "dma", "out", 128 * (hi - lo) * 4)

    ID, NID, IDB = ("idf", 0, 128), ("nidf", 0, 128), ("idb", 0, 128)
    tag[1] = -3.0
    load("s", ("3", "dli", 0, 24), "dl", 0, 192, "l_dl", 4)
    load("y", ("nti", 0, 24), "nt", 0, 24, "l_n0", 4)
    load("y", ("rb", 0, 2048), "r0", 0, 2048, "l_rb", 2)
    if C["wl"]:
        for a, b, z in ((0, NB, 0), (NB, 384, 2)):
            for k in range(8):
                load("y" if k % 2 or z else "s", ("wb", 384 * k + a, 384 * k + b), "w0", 384 * k + a, 384 * k + b, "l_w%d" % (z + k // 4), 2)
            if z == 0:
                load("y", ("db", 0, 384), "d0", 0, 384, "l_d0", 2)
                load("y", ("qui", 0, 72), "qu", 0, 72, "l_qu", 4)
    else:
        load("s", ("qui", 0, 72), "qu", 0, 72, "l_qu", 4)
        for i in range(4):
            load("y", ("wb", 768 * i, 768 * i + 768), "w0", 768 * i, 768 * i + 768, "l_w%d" % i, 2)
        load("y", ("db", 0, 384), "d0", 0, 384, "l_d0", 2)
    load("y", ("nti", 24, 120), "nt", 24, 120, "l_nt", 4)
    load("y", ("db", 384, 1920), "d0", 384, 1920, "l_d1", 2)
    tag[1] = -2.0
    iota(("pj", 0, 1), [[0, 1]], 0, 1)
    iota(("ld", 0, H * LC), [[LC, H], [24, 2], [0, LC // 2]], 0, 0)
    ts(("pk", 0, 1), ("pj", 0, 1), 15, None, A.bitwise_and)
    JF = ("jf", 0, 1)
    if LC == 8:
        ts(("pk", 1, 2), ("pj", 0, 1), 7, None, A.bitwise_and)
        cp(("jf", 0, 2), ("pk", 0, 2))
        ts(("ll", 0, H * LC), ("ld", 0, H * LC), ("jf", 1, 2), None, A.add)
    else:
        cp(("jf", 0, 1), ("pk", 0, 1))
        iota(("lb", 0, H * LC), [[0, H], [16, LC]], 0, 0)
        ts(("lb", 0, H * LC), ("lb", 0, H * LC), JF, None, A.add)
        ts(("lc", 0, H * LC), ("lb", 0, H * LC), 0.5 - LC / 2.0, 1.0 / LC, A.add, A.mult)
        ts(("le", 0, H * LC), ("lc", 0, H * LC), -float(LC), None, A.mult)
        tt(("lb", 0, H * LC), ("lb", 0, H * LC), ("ld", 0, H * LC), A.add)
        tt(("lb", 0, H * LC), ("lb", 0, H * LC), ("le", 0, H * LC), A.add)
        cp(("ll", 0, H * LC), ("lb", 0, H * LC))
    tag[1] = -0.5
    ms(("ones", 0, 256), 1.0)
    sel(("idf", 0, 256), ("ones", 0, 256), [[0, 2], [-1, 128]], A.is_equal, 0, 1)
    scp(("idb", 0, 256), ("idf", 0, 256))
    act(("nidf", 0, 256), ("idf", 0, 256), F.Copy, scale=-1.0)
    tag[1] = 0.1
    act(("i64", 0, 128), ID, F.Copy, scale=0.015625)
    act(("i8", 0, 128), ID, F.Copy, scale=-8.0)
    act(("idn", 0, 128), ID, F.Copy, scale=-4.0 * NB)
    if C["mod"]:
        act(("idk", 0, 128), ID, F.Copy, scale=-1024.0)
        ms(("kil", 0, LW), -1.0)
    ms(("t8a", 0, 8), 8.0 * TIE)
    ms(("z2", 0, 144), 0.0)
    sel(("t8b", 0, 8), ("t8a", 0, 8), [[-16, 8]], A.is_ge, 0, 1)
    sel(("t8c", 0, 8), ("t8b", 0, 8), [[16, 8]], A.is_ge, 15, -1)
    cp(("z2", 15, 143, 16), ("t8c", 0, 8))
    iota(("eca", 0, LW), [[0, LC], [NB - TIE, 8]], 7 * TIE, 0)
    iota(("eca", LW, 2 * LW), [[0, LC], [-TIE, 8]], 7 * TIE + 4 * NB, 0)
    sel(("keep", 0, 2 * LW), ("ones", 0, 2 * LW), [[0, 2 * LC], [1, 8]], A.is_gt, 0, 0)
    iota(("e2", 0, LW), [[16, LC], [0, 8]], 0, 0)
    act(("ecb", 0, LW), ("e2", 0, LW), F.Identity, bias=JF)
    iota(("le", 0, LC // 2), [[2, LC // 2]], 0, 0)
    ts(("pk", 2, 3), ("pj", 0, 1), 7, None, A.bitwise_and)
    ts(("pk", 3, 4), ("pj", 0, 1), 3, 1, A.logical_shift_right, A.bitwise_and)
    ts(("jg", 0, 1), ("pk", 2, 3), float(LC), None, A.mult)
    tt(("jg", 1, 2), ("jg", 0, 1), ("pk", 3, 4), A.add)
    ts(("turn", 0, LC // 2), ("le", 0, LC // 2), ("jg", 1, 2), None, A.add)
    iota(("e3", 0, LW), [[NB, 8], [16, LC]], 0, 0)
    act(("offc", 0, LW), ("e3", 0, LW), F.Identity, bias=JF)
    tag[1] = -1.5
    iota(("za", 0, 128), [[1, 128]], -9215827 - 64, 0)
    act(("za", 0, 128), ("za", 0, 128), F.Copy, scale=2.0 ** -23)
    act(("zb", 0, 128), ("za", 0, 128), F.Sigmoid)
    ops[-1]["cost"] += 1570
    ops[-1]["raw"] += 1570
    tag[1] = 0.1
    ts(("zb", 0, 128), ("zb", 0, 128), 0.25, None, A.is_equal)
    tt(("zb", 0, 128), ("zb", 0, 128), ("za", 0, 128), A.mult)
    add("v", lambda q, T, X: q.tensor_reduce(T.jf[:, 2:3], T.zb[:, :], AxisListType.X, A.min), [("jf", 2, 3)], [("zb", 0, 128)], 128)
    act(("quart", 0, NB), ("ones", 0, NB), F.Copy, scale=("jf", 2, 3))
    tag[1] = C["rr"]
    for z in range(0, 2048, 1024):
        scp(("rr", z, z + 1024), ("rb", z, z + 1024))
    tag[1] = -1.0
    cp(("cd", 0, 24), ("nti", 0, 24))
    tag[1] = 0.1
    cp(("cd", 24, 48), ("qui", 0, 24))
    ts(("3", "vall", 0, 24), ("3", "dli", 0, 24), -1.0, None, A.mult)
    cp(("qa", 0, 72), ("qui", 0, 72))
    cp(("ntu", 0, 120), ("nti", 0, 120))

    def heads(s):
        o = (s + 1) * 48
        if s == S - 1:
            scp(("cd", o, o + 24), ("qa", s * 24, s * 24 + 24))
            return
        tt(("cd", o, o + 24), ("nti", s * 24 + 24, s * 24 + 48), ("qa", s * 24, s * 24 + 24), A.subtract)
        tt(("cd", o + 24, o + 48), ("qa", s * 24 + 24, s * 24 + 48), ("qa", s * 24, s * 24 + 24), A.subtract)

    TB, T0 = "py", 384

    def sums(s0, s1):
        lo, hi = (s0 + 1) * 24, (s1 + 1) * 24
        o = (TB, T0, T0 + hi - lo)
        a = max(s0, 0)
        it = [(o, ID, ("k", "vall", k, lo, hi), k == 0, False) for k in range(8)]
        it.append(((TB, T0 + (a - s0) * 24, T0 + hi - lo), ("i8", 0, 128), ("qa", a * 24, s1 * 24), False, True))
        for z in range(0, 9, 3):
            mm(it[z:z + 3], TB)
        scp(("gs", lo, hi), o)

    def tails(s0, s1):
        o = (TB, T0, T0 + 24 * (s1 - s0))
        mm([(o, ID, ("qa", s0 * 24, s1 * 24), True, False), (o, NID, ("gs", s0 * 24, s1 * 24), False, False),
            (o, ID, ("gs", s0 * 24 + 24, s1 * 24 + 24), False, True)], TB)
        scp(("qa", s0 * 24 + 72, s1 * 24 + 72), o)

    XP = 4 if C["x_by"] == "v" else 3

    def lists(s, h):
        c = (s + 1) * 24 + LC * h
        return ("3", "vall", c, c + LC), ("pv", 2 * LW, 3 * LW), ("pv", (XP + h) * LW, (XP + h + 1) * LW)

    def post(s, h):
        n = "_%d" % h
        v, cb, xp = lists(s, h)
        o = (s + 1) * 48
        if s == S - 1:
            scp(("bc" + n, 0, LW), ("i", ("cd", o, o + 24), ("ll", LC * h, LC * h + LC // 2)))
            tt(("3", "yds", LC * h, LC * h + LC), ("bc" + n, 0, LW), v, A.subtract)
            return
        scp(("bc" + n, 0, 2 * LW), ("i", ("cd", o, o + 48), ("ll", LC * h, LC * h + LC)))
        if s >= 0 and C["mod"]:
            it = [(cb, ID, ("bc" + n, 0, LW), True, False), (cb, ID, v, False, True)]
            mm(it, "pv")
            ops[-1]["cls"] = "t:u"
            act(("su" + n, 0, LW), cb, F.Sign, bias=0.5)
            mm(it[:1] + [(cb, ID, v, False, False), (cb, ("idk", 0, 128), ("kil", 0, LW), False, False), (cb, ("idk", 0, 128), ("su" + n, 0, LW), False, True)], "pv")
            ops[-1]["cls"] = "t:u"
            cp(("off" + n, 0, LW), cb)
        else:
            if s < 0:
                tag[1] = -1.0 + 0.4 * h
                cp(("nh" + n, 0, LW), ("3", "dli", LC * h, LC * h + LC))
                tt(("ui" + n, 0, LW), ("i", ("cd", 0, 24), ("ll", LC * h, LC * h + LC // 2)), ("nh" + n, 0, LW), A.subtract)
            elif C["x_by"] == "t":
                scp(cb, ("bc" + n, 0, LW))
                tt(("ui" + n, 0, LW), cb, v, A.add)
            else:
                scp(("pv", 2 * LW, 4 * LW), ("bc" + n, 0, 2 * LW))
                tt(("ui" + n, 0, LW), cb, v, A.add)
            ts(("uj" + n, 0, LW), ("ui" + n, 0, LW), 2047, None, A.bitwise_and)
            cp(("off" + n, 0, LW), ("uj" + n, 0, LW))
        if C["x_by"] == "t":
            mm([(xp, ID, ("bc" + n, LW, 2 * LW), True, False), (xp, ID, v, False, True)], "pv")
        elif s < 0:
            tt(xp, ("bc" + n, LW, 2 * LW), v, A.add)
        else:
            tt(xp, ("pv", 3 * LW, 4 * LW), v, A.add)
        act(("aa" + n, 0, LW), xp, F.Abs)
        act(("ab" + n, 0, LW), ("i", ("aa" + n, 0, LW), ("turn", 0, LC // 2)), F.Abs, bias=-1024.0)
        act(("sg" + n, 0, LW), ("ab" + n, 0, LW), F.Sign, bias=-511.5)

    def bank(kind, s, h, lo, hi):
        c = lo // BW
        return ("%s_%d" % (kind, (NBK * (H * s + h) + c) % 2), lo - BW * c, hi - BW * c)

    def late(s, h, lo):
        return s == 0 and lo < C["direct"][h]

    def wb_pieces(h, lo, hi):
        cut = sorted(set([lo, hi] + [z for z in range(0, WP, NB) if lo < z < hi]))
        return [(a, b, ("wb", (a // NB) * 384 + NB * h + a % NB, (a // NB) * 384 + NB * h + a % NB + b - a)) for a, b in pairs(cut)]

    def wb_load(kind, h, lo, hi, stop):
        mm([(bank(kind, 0, h, a, b), IDB, z, a == lo, stop and b == hi) for a, b, z in wb_pieces(h, lo, hi)], bank(kind, 0, h, lo, hi)[0])

    def acc(s, h):
        z = "pl_%d" % ((H * s + h) % 2 if H > 2 else 0)
        return ("k", z, 0, 0, 2 * NB), ("k", z, 1, 0, 2 * NB)

    def places(s, h):
        if H > 2:
            z = (H * s + h) % 2
            e = {"pl": acc(s, h)[0], "py": ("py", 2 * NB, 3 * NB), "pv": ("pv", 384, 512)}[C["e_at"]]
            return ("py", NB * z, NB * z + NB), e, acc(s, h)[1]
        y = ("k", "pl_0", 0, 0, NB) if (s, h) == (0, 1) else ("py", 0, NB)
        return y, ("py", BW - 2 * NB, BW), bank("st", s, h, BW, BW + 2 * NB)

    def blocks(h):
        return C["send"][h], C["send"][h + 1]

    def front(s, h):
        n = "_%d" % h
        phase("front", s, h)
        y, e, _ = places(s, h)
        r = 16 * (1 + s)
        c0 = s * 384 + NB * h
        win = ("rb", 0, 2048) if s == 0 else ("rr", 0, 2048)
        for i, (lo, hi) in enumerate(pairs(C["gb"])):
            (cp if s == 0 and i in C["v_gath"][h] else scp)(("x" + n, lo, hi), ("i", win, ("off" + n, lo // 16, hi // 16)))
        k = 0
        for lo, hi in pairs(C["pb"]):
            if late(s, h, lo):
                for a, b, z in wb_pieces(h, lo, hi):
                    tt(("p" + n, a, b), ("x" + n, a, b), z, A.mult)
            else:
                if lo % BW == 0 and s > 0:
                    scp(bank("st", s, h, lo, lo + BW), ("w" + n, lo, lo + BW))
                elif lo % BW == 0:
                    wb_load("st", h, lo, lo + BW, True)
                tt(("p" + n, lo, hi), bank("st", s, h, lo, hi), ("x" + n, lo, hi), A.mult)
            it = []
            while NB * k + NB <= hi:
                it.append((y, ("nidf", 128 - r, 256 - r), ("p" + n, NB * k, NB * k + NB), k == 0, False))
                k += 1
            if k == 8:
                it.append((y, ("idb", 128 - r, 256 - r), ("db", c0, c0 + NB), False, True))
            if it:
                mm(it, regs(y)[0][0])
                ops[-1]["cls"] = "t:py"
        ts(("snd", c0, c0 + NB), y, -2.0, 2.0, A.max, A.min)
        lo, hi = blocks(h)
        if lo == hi:
            return

        def send(q, T, X):
            core, rank, topo = X
            tr = []
            for b in range(lo, hi):
                dst = T.cores[(rank + 1 + b) % len(T.cores)]
                rid, pid, _ = topo.addr(dst)
                eng = topo.engines(core, dst)
                share = len(eng) // (hi - lo)
                c = s * 384 + 96 * b
                tr.append(RemoteDMATransfer(dst_ids=[DstId(rid=rid, pnc=pid)], dma_engine_mask=sum(1 << j for j in eng[share * (b - lo):share * (b - lo + 1)]),
                                            remote_sem=T.sem["arr%d_%d" % (s, h)], src=T.snd[:, c:c + 96], dst=T.land[:, c:c + 96]))
            return q.remote_dma_fused(tr, local_sem=T.sem.sent)
        k = add("g", send, [], [("snd", s * 384 + 96 * lo, s * 384 + 96 * hi)], 360, "send")
        add(None, None, [("land", s * 384 + 96 * lo, s * 384 + 96 * hi)], [], 0, "recv", "arr%d_%d" % (s, h), after=k)

    ring = [1]

    def update(s, h):
        n = "_%d" % h
        phase("update", s, h)
        _, e, m0 = places(s, h)
        r, c0 = 16 * (1 + s), s * 384 + NB * h
        reps = C["erep"] if C["e_by"] == "t" else 1
        mm([(part(e, NB * z, NB * z + NB), ("idf", r, 128 + r), ("snd", c0, c0 + NB), z == 0, z == reps - 1) for z in range(reps)], regs(e)[0][0])
        ops[-1]["cls"] = "t:e"
        if reps < C["erep"]:
            scp(part(e, NB, 2 * NB), part(e, 0, NB))
            ops[-1]["cls"] = "s:e"
        wd = NB * C["erep"]
        for c in range(0, WP, wd):
            tt(("t" + n, c, c + wd), part(e, 0, wd), ("x" + n, c, c + wd), A.mult)
        cuts = [(BW * c, BW * c + BW, "T") for c in range(NBK)] if s == 0 else [z + (m,) for z, m in zip(pairs(C["ub"]), C["um"])]
        wd = NB * C["lanes"]
        taps = [(k + C["first"]) % 8 for k in range(8)]
        for lo, hi, mode in cuts:
            up, wv, tv = bank("up", s, h, lo, hi), ("w" + n, lo, hi), ("t" + n, lo, hi)
            if C["fix"] and s > 0:
                up = ("up_%d" % (ring[0] % 2), 0, hi - lo) if mode == "T" else bank("st", s, h, 0, hi - lo)
                ring[0] += mode == "T"
            if mode == "T":
                if s == 0:
                    wb_load("up", h, lo, hi, False)
                else:
                    mm([(up, ID, wv, True, False)], up[0])
                ops[-1]["cls"] = "t:load"
                mm([(up, ("i64", 0, 128), tv, False, True)], up[0])
                new = up
            elif mode == "D":
                act(tv, tv, F.Copy, scale=0.015625)
                ops[-1]["cls"] = "s:far"
                add("g", lambda q, T, X, a=wv, b=tv: q.dma_start(ap(T, a), ap(T, b), accum_op=A.add), [wv], [wv, tv], 1200, "dma",
                    "upd%d_%d" % (s, h), 2 * 128 * (hi - lo) * 4)
                new = wv
            else:
                act(up, tv, F.Copy, scale=0.015625)
                ops[-1]["cls"] = "s:up"
                tt(wv, up, wv, A.add)
                new = wv
            if lo <= NB * taps[0] < hi:
                act(part(m0, 0, wd), part(new, NB * taps[0] - lo, NB * taps[0] - lo + wd), F.Abs)
                ops[-1]["cls"] = "s:m0"
            for a, b in pairs(sorted(set([lo, hi] + [z for z in C["ab"] if lo < z < hi]))):
                act(("m" + n, a, b), part(new, a - lo, b - lo), F.Abs)
                if mode == "D":
                    ops[-1]["cls"] = "s:mfar"
            if mode == "T":
                scp(wv, up)
        phase("minmax", s, h)
        m = lambda k, z=1: ("m" + n, NB * k, NB * (k + z))
        both = list(zip(acc(s, h), (A.min, A.max)))
        if C["lanes"] == 1:
            for k in taps[1:]:
                for a, op in both:
                    tt(part(a, 0, NB), part(m0 if k == taps[1] else a, 0, NB), m(k), op)
        else:
            for k in (taps[2], taps[4]):
                for a, op in both:
                    tt(a, m0 if k == taps[2] else a, m(k, 2), op)
            for z, (a, op) in enumerate(both):
                tt(part(a, 0, NB), part(a, 0, NB), m(taps[6]), op)
                tt(("sb" + n, NB * z, NB * z + NB), part(a, NB, 2 * NB), m(taps[7]), op)
                ops[-1]["cls"] = "v:pl"
            for z, (a, op) in enumerate(both):
                tt(part(a, 0, NB), part(a, 0, NB), ("sb" + n, NB * z, NB * z + NB), op)
        if C["rep"] == 2:
            z = acc(s, h)[0][1]
            scp(("3", z, NB, 2 * NB), ("3", z, 0, NB))

    def vote(s, h):
        n = "_%d" % h
        phase("masks", s, h)
        wd = NB * C["rep"]
        for e in range(2):
            for k in range(8):
                tt(("c", "eq" + n, NB * e, NB * e + NB, k), part(acc(s, h)[e], 0, NB), ("m" + n, NB * k, NB * k + NB), A.is_equal)
        o = ("pv", 0, 2 * LW)
        it = [(o, IDB, ("eca", 0, 2 * LW), True, False), (("pv", 0, LW), IDB, ("ecb", 0, LW), False, False),
              (("pv", LW, 2 * LW), ("idn", 0, 128), ("sg" + n, 0, LW), False, False)]
        if C["base"]:
            mm(it, "pv")
            ops[-1]["cls"] = "t:base"
            it = []
        mm(it + [(o, ("z2", 15 - j, 143 - j), ("j", "eq" + n, j), False, j == 15) for j in range(16)], "pv")
        phase("lists", s, h)
        vec(lambda q, T, X: q.tensor_tensor_scan(T["ta" + n][:, :], T.keep[:, :], ap(T, o), 0.0, A.mult, A.max),
            ("ta" + n, 0, 2 * LW), [o, ("keep", 0, 2 * LW)])
        tt(("tc" + n, 0, LC), ("ta" + n, 7, LW, 8), ("ta" + n, LW + 7, 2 * LW, 8), A.add)
        ts(("gg" + n, 0, LC), ("tc" + n, 0, LC), TIE - 1, None, A.bitwise_and)
        cp(("wo" + n, 0, LC), ("gg" + n, 0, LC))
        act(("i", ("w" + n, 0, 2 * WP), ("wo" + n, 0, LC)), ("quart", 0, NB), F.Sigmoid)
        tt(("nh" + n, 0, LW), ("i", ("gg" + n, 0, LC), ("ll", 0, LC // 2)), ("offc", 0, LW), A.not_equal)
        v, _, xp = lists(s, h)
        tt(v, xp, ("nh" + n, 0, LW), A.mult)
        post(s, h)

    def scatter(s):
        for h in range(H):
            phase("scatter", s, h)
            lo, hi = blocks(h)
            if lo < hi:
                cp(("i", ("rr", 0, 2048), ("ntu", s * 24 + 6 * lo, s * 24 + 6 * hi)), ("land", s * 384 + 96 * lo, s * 384 + 96 * hi))

    for h in range(H):
        post(-1, h)
    tag[1] = 0.1
    heads(0)
    heads(1)
    for s in range(S):
        for h in range(H):
            if (s, h) == (0, 0):
                front(0, 0)
                front(0, 1)
            update(s, h)
            if h == H - 1 and s < S - 1:
                scatter(s)
                front(s + 1, 0)
            elif h < H - 1 and (s, h) != (0, 0):
                front(s, h + 1)
            if h == 0 and s in (2, 4):
                phase("tails", s, h)
                sums(-1 if s == 2 else 2, s)
                tails(s - 2, s)
                if s == 2:
                    for z in (2, 3, 4):
                        heads(z)
            vote(s, h)
    tag[:] = ["end", 1000.0]
    for h in range(H):
        for k in range(8):
            store("y" if h < H - 1 or k % 2 else "s", "yw", k * 384 + NB * h, k * 384 + NB * h + NB, ("w_%d" % h, NB * k, NB * k + NB))
    store("y", "yr", 0, 384, ("land", 1536, 1920))
    o = ("up_0", 0, 24)
    mm([(o, ID, ("qa", 96, 120), True, False), (o, ("i8", 0, 128), ("qa", 96, 120), False, False), (o, NID, ("gs", 96, 120), False, False)], "up_0")
    mm([(o, ID, ("k", "vall", k, 120, 144), False, k == 7) for k in range(8)], "up_0")
    scp(("qa", 168, 192), o)
    store("y", "yd", 0, 192, ("3", "yds", 0, 24))
    store("s", "yq", 0, 72, ("qa", 120, 192))
    return ops


def edges(ops):
    n = len(ops)
    pred = [set() for _ in range(n)]
    hist = {}
    for i, o in enumerate(ops):
        if o["after"] is not None:
            pred[i].add(o["after"])
        for rg, w in [(r, False) for r in o["rd"]] + [(r, True) for r in o["wr"]]:
            for j, lo, hi, w2 in hist.get(rg[0], []):
                if (w or w2) and lo < rg[2] and rg[1] < hi and j != i:
                    pred[i].add(j)
        for rg in o["wr"]:
            hist[rg[0]] = [z for z in hist.get(rg[0], []) if not (rg[1] <= z[1] and z[2] <= rg[2])]
        for rg, w in [(r, False) for r in o["rd"]] + [(r, True) for r in o["wr"]]:
            hist.setdefault(rg[0], []).append((i, rg[1], rg[2], w))
    succ = [[] for _ in range(n)]
    for i in range(n):
        for j in pred[i]:
            succ[j].append(i)
    return pred, succ


def schedule(ops, data):
    n = len(ops)
    C = CFG
    lam = C["lam"]
    pred, succ = [set(p) for p in data[0]], data[1]
    cost = [o["cost"] * C["cy"] + (C["ovh"] if o["eng"] in ("v", "s") else C["tovh"] * o["nins"] if o["eng"] == "t" else 0.0) for o in ops]
    prio, seen = [], {}
    for i, o in enumerate(ops):
        z = o["tag"].split()
        if len(z) == 1:
            prio.append(-(10 * o["ph"] + 1e-4 * i))
            continue
        k = seen[o["tag"], o["cls"]] = seen.get((o["tag"], o["cls"]), -1) + 1
        at = C["round"].get(z[0] + " " + o["cls"], C["round"][z[0]])
        at += C["pace"].get(z[0] + " " + o["cls"], C["pace"].get(z[0], 0.0)) * k + C["shift"][z[0]][int(z[2])]
        if z[1] in "04":
            at += C["shift"].get(z[0] + z[1], [0.0] * H)[int(z[2])]
        prio.append(-(C["step"] * int(z[1]) + at + 1e-4 * i))
    line = {e: sorted((i for i in range(n) if ops[i]["eng"] == e and ops[i]["tag"] != "start"), key=lambda z: prio[z]) for e in C["win"]}
    done = set()
    left = [len(p) for p in pred]
    ready = {e: [i for i in range(n) if left[i] == 0 and ops[i]["eng"] == e] for e in ("v", "s", "t", "g", "y", None)}
    free = {e: 0.0 for e in ready}
    fin, start, base = [0.0] * n, [0.0] * n, [0.0] * n
    bank, order, wire, busy = {}, [], 0.0, set()

    def when(i):
        e0 = ops[i]["eng"]
        t = max(free[e0], base[i])
        for b in ops[i]["banks"]:
            for e, j in bank.get(b, {}).items():
                if e != e0 and fin[j] + lam > t:
                    t = fin[j] + lam
        return t
    for _ in range(n):
        best = None
        for e, lst in ready.items():
            if e == "t":
                lst = [i for i in lst if not (ops[i]["group"][1] and ops[i]["group"][0] in busy)]
            if line.get(e):
                least = prio[line[e][-1]] - C["win"][e]
                lst = [i for i in lst if prio[i] >= least or ops[i]["tag"] == "start"]
            if lst:
                can = [(when(i), i) for i in lst]
                if best is None or min(can)[0] < best[0]:
                    best = (min(can)[0], e, can)
        if best is None:
            i = max((i for e, lst in ready.items() for i in lst if e != "t"), key=lambda z: prio[z])
            best = (when(i), ops[i]["eng"], [(when(i), i)])
        t0, e0, can = best
        _, i, t = min((-prio[i], i, t) for t, i in can if t <= t0 + C["look"].get(e0, 0.0))
        o = ops[i]
        ready[e0].remove(i)
        if e0 == "t":
            (busy.discard if o["group"][2] else busy.add)(o["group"][0])
        done.add(i)
        while line.get(e0) and line[e0][-1] in done:
            line[e0].pop()
        for b in o["banks"]:
            for e, j in bank.setdefault(b, {}).items():
                if e != o["eng"]:
                    pred[i].add(j)
            bank[b][o["eng"]] = i
        start[i] = t
        fin[i] = t + cost[i]
        if o["eng"] is not None:
            free[o["eng"]] = fin[i]
        if o["kind"] == "dma":
            wire = max(wire, fin[i] + 1500) + o["bytes"] / 180.0
            fin[i] = wire + 500
        if o["kind"] == "recv":
            fin[i] += C["rem"]
        order.append(i)
        for j in succ[i]:
            base[j] = max(base[j], fin[i] + (0.0 if e0 == "t" and ops[j]["eng"] == "t" else lam))
            left[j] -= 1
            if left[j] == 0:
                ready[ops[j]["eng"]].append(j)
    return order, pred, start, fin


def waits(ops, order, pred):
    seq, known, clock, need, raised = {}, {e: {} for e in "vstgy"}, {}, {}, set()
    at = {}
    for i in order:
        o = ops[i]
        e = o["eng"]
        if o["kind"] == "recv":
            clock[i] = {}
            at[i] = (o["sem"], 1)
            continue
        kn = known[e]
        lst = []
        for j in sorted(pred[i], key=lambda z: -at[z][1]):
            if e == "t" and ops[j]["eng"] == "t":
                continue
            key, val = at[j]
            if kn.get(key, 0) >= val:
                continue
            lst.append(j)
            kn[key] = val
            for k2, v2 in clock[j].items():
                if kn.get(k2, 0) < v2:
                    kn[k2] = v2
        need[i] = lst
        raised.update(lst)
        clock[i] = dict(kn)
        if o["kind"] == "c":
            seq[e] = seq.get(e, 0) + 1
            at[i] = (e, seq[e])
        else:
            at[i] = ("op%d" % i, 1)
    count, val = {}, {}
    for i in order:
        o = ops[i]
        if o["kind"] == "c" and i in raised:
            count[o["eng"]] = count.get(o["eng"], 0) + 1
            val[i] = (ESEM[o["eng"]], count[o["eng"]])
        elif o["kind"] == "dma":
            val[i] = (o["sem"], 16 * sum(z["sem"] == o["sem"] for z in ops))
        elif o["kind"] == "recv":
            val[i] = (o["sem"], 16)
    return need, val


PLAN = {}


def plan():
    if not PLAN:
        ops = program()
        order, pred, start, fin = schedule(ops, edges(ops))
        need, val = waits(ops, order, pred)
        PLAN.update(ops=ops, order=order, need=need, val=val, start=start, fin=fin, pred=pred)
    return PLAN


def rank_program(g, core, T, topo):
    rank = T.rank_of(core)
    if rank is None:
        return
    P = plan()
    ops, need, val = P["ops"], P["need"], P["val"]
    Q = {"v": g.vector, "s": g.scalar, "t": g.tensor, "g": g, "y": g.sync}
    X = (core, rank, topo)
    stores = 0
    for i in P["order"]:
        o = ops[i]
        if o["kind"] == "recv":
            continue
        q = Q[o["eng"]]
        for name, count in sorted(set(val[j] for j in need[i])):
            q.wait_ge(T.sem[name], count)
        ins = o["fn"](q, T, X)
        if o["kind"] == "dma":
            ins.then_inc(T.sem[o["sem"]], 16)
            stores += o["sem"] == "out"
        elif i in val and o["kind"] == "c":
            ins.then_inc(T.sem[val[i][0]], 1)
    g.wait_ge(T.sem.sent, 16 * sum(o["kind"] == "send" for o in ops))
    g.wait_ge(T.sem.out, 16 * int(stores))
